import numpy as np, ml_dtypes
CORES = [48,51,52,55]
N = 4
BF = ml_dtypes.bfloat16
P, T, WR, H, VIS, MT, LP = 4096, 1024, 256, 2048, 2, 3, 12
lev = np.arange(16)[:, None]
def parts(rng, step=2):
    p = np.arange(P); bit = 1 << np.maximum(LP - 1 - lev, 0); base = rng.integers(1, 3, (1, 8, 16, 1)); s = []
    for n in (P, T):
        flip = rng.random((N, 8, 16, n), dtype=np.float32) < rng.choice(np.array([0.02, 0.1, 0.3]), (N, 8, 1, n))
        s.append(np.where(flip, 3 - base, base))
    b, a = s; tree = 1 + ((p[None, :] & bit) > 0).astype(np.int64)
    start = rng.integers(0, P, (N, len(range(0, 8, step)), T))
    b[:, ::step] = np.where(lev < LP, tree, b[:, ::step])
    a[:, ::step] = np.where(lev < LP, np.moveaxis(tree[:, start], 0, 2), a[:, ::step])
    u = rng.random((N, 8, 16, P)); R = np.where(rng.random((N, 8, 16, P), dtype=np.float32) < 0.5, rng.integers(0, P, (N, 8, 16, P)), (P * u * u * u).astype(np.int64))
    near = ((p[None, :] ^ bit) & -bit) | (R[:, ::step] & (bit - 1))
    R[:, ::step] = np.where(lev < LP, near, R[:, ::step])
    E = rng.integers(0, 16, (N, 8, 16, P)); D = rng.integers(0, 16, (N, 8, 16, T))
    return b, E, R, a, D, rng.integers(0, 256, (N, 8, 16, 1)), rng.integers(60, 111, (N, 8, 16, 1))
def cut(s, n, h):
    return np.where((lev < n) & (lev != h), s, 0)
def cuts(rng, b, a):
    nb = np.maximum(rng.integers(0, 17, (N, 8, 1, P)), rng.integers(0, 17, (N, 8, 1, P))); na = rng.integers(0, 17, (N, 8, 1, T))
    nb[:, 1::2] = 4 * rng.integers(0, 5, (N, 4, 1, P)); na[:, 1::2] = 4 * rng.integers(0, 5, (N, 4, 1, T))
    return cut(b, nb, rng.integers(0, 32, (N, 8, 1, P))), cut(a, na, rng.integers(0, 24, (N, 8, 1, T)))
def pack(b, E, R, a, D, w, t):
    return {"peers": np.ascontiguousarray((b + 4 * E + 64 * R).reshape(N, 128, P)).astype(np.int32), "trav": np.ascontiguousarray((a + 4 * D).reshape(N, 128, T)).astype(np.float32).astype(BF),
            "wts": np.ascontiguousarray(w.reshape(N, 128, 1)).astype(np.int32), "th": np.ascontiguousarray(t.reshape(N, 128, 1)).astype(np.int32)}
def setup_inputs(rng):
    b, E, R, a, D, w, t = parts(rng); b, a = cuts(rng, b, a)
    return pack(b, E, R, a, D, w, t)
def setup_inputs_alone(rng):
    b, E, R, a, D, w, t = parts(rng)
    full = b[:, 1::4, :, 0].copy(); b, a = cuts(rng, b, a); b[:, 1::4, :, 0] = full
    w[:, ::2] = 0; w[:, ::2, 0] = 1; w[:, ::2, 1] = 16; t[:, ::2] = 241
    for q in range(N):
        for g in range(0, 8, 2):
            x = np.concatenate([rng.permutation(256) for i in range(T // 256)])
            D[q, g, 0] = x & 15; D[q, g, 1] = x >> 4; R[q, g] = rng.permutation(P)[None, :]
    three = rng.integers(0, 16, (N, 4, 16, 3)); D[:, 1::2] = np.take_along_axis(three, rng.integers(0, 3, (N, 4, 1, T)), 3)
    w[:, 1::4] = 0; R[:, 3::4] = rng.choice(np.array([0, P - 1, 5, P // 2]), (N, 2, 16, P))
    return pack(b, E, R, a, D, w, t)
def setup_inputs_ties(rng):
    b, E, R, a, D, w, t = parts(rng)
    b = cut(b, rng.integers(0, 3, (N, 8, 1, P)), 99); a = cut(a, rng.integers(0, 3, (N, 8, 1, T)), 99)
    v = rng.integers(1, 15, (8, 16)); o = np.argsort(rng.random((N, 8, 16, T)), axis=2)
    D = np.take_along_axis(v[None, :, :, None], o, 2)
    D = D + (lev == rng.integers(0, 16, (N, 8, 1, T))) * rng.integers(-1, 2, (N, 8, 1, T))
    E[:, ::2] = 0; E[:, 1::2] = 15; s = np.add.reduce(v, axis=1)
    t[:] = np.where(np.arange(8) % 2 == 0, s, 240 - s)[None, :, None, None]
    return pack(b, E, R, a, D, w, t)
def setup_inputs_ends(rng):
    b, E, R, a, D, w, t = parts(rng); b, a = cuts(rng, b, a); o = rng.permutation(8); base = rng.integers(1, 3, (16, 1))
    for i in (0, 1, 4, 5): a[:, o[i]] = base
    for i in (0, 1, 4, 5, 6): b[:, o[i]] = base
    a[:, o[1]] = np.where(lev == 15, rng.integers(0, 3, (N, 1, T)), base); b[:, o[1]] = np.where(lev == 15, rng.integers(0, 3, (N, 1, P)), base)
    a[:, o[2:4]] = 0; b[:, o[2:4]] = 0
    b[:, o[4]] = np.where(lev == 0, 3 - base, base); b[:, o[5]] = np.where(lev == 15, 0, base)
    a[:, o[6]] = np.where(lev == 0, 0, base); b[:, o[6]] = np.where(lev == 0, rng.integers(1, 3, (N, 1, P)), base)
    R[:, o[:4]] = np.where(rng.random((N, 4, 16, P)) < 0.5, R[:, o[:4]], rng.choice(np.array([0, P - 1]), (N, 4, 16, P)))
    x = np.stack([np.concatenate([rng.permutation(256) for i in range(T // 256)]) for q in range(2 * N)]).reshape(2, N, 1, T); z = np.arange(256)[None, :]
    h, k, n = int(o[2]), int(o[3]), int(o[7]); v = rng.integers(0, 16, (16, 1)); sh = np.minimum(lev, 7)
    t[:, h] = 0; w[:, h] = np.where(lev == 0, 1, np.where(lev == 1, 16, 0))
    D[:, h] = np.where(lev == 0, x[0] & 15, np.where(lev == 1, x[0] >> 4, v)); E[:, h, :, :256] = np.where(lev == 0, z & 15, np.where(lev == 1, z >> 4, v))
    t[::2, k] = 241; t[1::2, k] = 240; w[:, k] = np.where(lev < 8, 1 << sh, 0)
    D[:, k] = 15 * np.where(lev < 8, (x[1] >> sh) & 1, 1)
    there = E[:, k]; there[:, :, (15 * z[0]) & (P - 1)] = 15 - 15 * np.where(lev < 8, (z >> sh) & 1, 1)
    w[:, n] = rng.integers(240, 256, (N, 16, 1)); D[:, n] = rng.integers(13, 16, (N, 16, T))
    return pack(b, E, R, a, D, w, t)
def setup_inputs_grid(rng):
    b, E, R, a, D, w, t = parts(rng, 1); p = np.arange(P)[None, :]
    b = cut(b, 16, rng.integers(0, 64, (N, 8, 1, P))); a = cut(a, rng.integers(6, 17, (N, 8, 1, T)), rng.integers(0, 5, (N, 8, 1, T)))
    late = (lev >= 12) & (lev < 15); bit = 1 << np.clip(lev - 12, 0, 2); low = (p & (bit - 1)) | ((p ^ bit) & bit)
    for i in rng.permutation(8)[:2]:
        g = int(i); base = rng.integers(1, 3, (16, 1))
        b[:, g] = np.where(lev == 15, rng.integers(1, 3, (N, 1, P)), np.where(late & ((p & bit) > 0), 3 - base, base))
        hole = (lev == rng.integers(12, 15, (N, 1, T))) | (lev == rng.choice(np.array([12, 13, 14, 99, 99, 99]), (N, 1, T)))
        a[:, g] = np.where(hole, 0, np.where(lev == 15, rng.integers(1, 3, (N, 1, T)), base))
        R[:, g] = np.where(late, (R[:, g] & -8) | low, R[:, g])
    return pack(b, E, R, a, D, w, t)
def setup_inputs_spread(rng):
    b, E, R, a, D, w, t = parts(rng)
    u = rng.random((N, 8, 1, P)); b = np.where(rng.random((N, 8, 16, P)) < u * u, 0, b)
    u = rng.random((N, 8, 1, T)); a = np.where(rng.random((N, 8, 16, T)) < u * u, 0, a)
    u = rng.random((N, 8, 1, P)); E = (16 * rng.random((N, 8, 16, P)) * u * u).astype(np.int64)
    u = rng.random((N, 8, 1, T)); D = (16 * rng.random((N, 8, 16, T)) * u * u).astype(np.int64)
    R = np.minimum(np.exp2(LP * rng.random((N, 8, 16, P))).astype(np.int64), P) - 1; R[:, 1::2] = P - 1 - R[:, 1::2]
    w = np.minimum(np.exp2(8 * rng.random((N, 8, 16, 1))).astype(np.int64), 255) * (rng.random((N, 8, 16, 1)) > 0.125)
    return pack(b, E, R, a, D, w, rng.integers(0, 242, (N, 8, 16, 1)))
def check_inputs(d):
    bad = []
    for k, hi in (("peers", 64 * P - 1), ("wts", 255), ("th", 241)):
        if np.min(d[k]) < 0 or np.max(d[k]) > hi: bad.append("range of " + k)
    if np.any((np.asarray(d["peers"]).astype(np.int64) & 3) == 3): bad.append("symbols of peers")
    t = np.asarray(d["trav"]).astype(np.float64)
    if not np.all((t >= 0) & (t <= 62) & (t == np.floor(t))): bad.append("range of trav")
    if np.any(t - 4 * np.floor(t * 0.25) == 3): bad.append("symbols of trav")
    return bad
def reference(peers, trav, wts, th):
    c = peers.astype(np.int32).reshape(N, 8, 16, P); B = c & 3; E = (c >> 2) & 15; R = c >> 6
    t = trav.astype(np.float32).astype(np.int32).reshape(N, 8, 16, T); a = t & 3; D = t >> 2
    w = wts.astype(np.int32).reshape(N, 8, 16, 1); lim = th.astype(np.int32).reshape(N, 8, 16, 1)
    below = np.arange(WR)[None, :] < np.arange(WR)[:, None]
    for visit in range(VIS):
        if visit: a = np.roll(a, 1, axis=0); D = np.roll(D, 1, axis=0)
        G = np.full(a.shape, -1, np.int32)
        m = (np.add.reduce(w * D, axis=2) & (P - 1)).astype(np.int64)
        for meeting in range(MT):
            ix = m[:, :, None, :]
            b = np.take_along_axis(B, ix, 3); e = np.take_along_axis(E, ix, 3); r = np.take_along_axis(R, ix, 3)
            part = (a != b) | (a == 0) | (b == 0)
            l = np.where(np.any(part, axis=2), np.argmax(part, axis=2), 15)[:, :, None, :]
            at = lev == l
            al = np.take_along_axis(a, l, 2); bl = np.take_along_axis(b, l, 2); rl = np.take_along_axis(r, l, 2); tl = np.take_along_axis(lim, l, 2)
            far = np.add.reduce(np.abs(D - e), axis=2)[:, :, None, :]
            s = m[:, :, :WR]; twin = np.any((s[..., :, None] == s[..., None, :]) & below, axis=3)
            wr = np.zeros((N, 8, T), bool); wr[:, :, :WR] = ~twin; wl = wr[:, :, None, :]
            c1 = wl & (al == 0) & (bl == 0) & (far >= tl); c2 = (al == 0) & (bl != 0)
            c3 = wl & (al != 0) & (bl == 0); c4 = wl & (al != 0) & (bl != 0) & (al != bl)
            swap = c4 & (lev < l) & (G >= 0)
            na = np.where(at & c1, 1, np.where(at & c2, 3 - b, a)).astype(np.int32)
            nb = np.where(at & c1, 2, np.where(at & c3, 3 - a, b)).astype(np.int32)
            nd = np.where(c1, np.maximum(D, e), D); ne = np.where(c1, np.minimum(D, e), e)
            nr = np.where((at & c3 & (G >= 0)) | swap, G, r)
            ng = np.where(at & (c1 | c2), ix, np.where(swap, r, G)).astype(np.int32)
            for q in range(N):
                for g in range(8):
                    j = np.flatnonzero(wr[q, g]); p = m[q, g, j]
                    B[q, g][:, p] = nb[q, g][:, j]; E[q, g][:, p] = ne[q, g][:, j]; R[q, g][:, p] = nr[q, g][:, j]
            a, D, G = na, nd, ng; m = rl[:, :, 0, :].astype(np.int64)
    yp = (B + 4 * E + 64 * R)[..., :H]
    return {"yp": np.ascontiguousarray(yp.reshape(N, 128, H)).astype(np.float32), "yt": np.ascontiguousarray((a + 4 * D).reshape(N, 128, T)).astype(np.float32).astype(BF)}

@@ -1,0 +1,562 @@
+from concourse.bass import DstId, RemoteDMATransfer
+from concourse.mybir import AluOpType as A, ActivationFunctionType as F, AxisListType as AX
+
+CFG = {"cyc": 1.04, "pe": 0.52, "gat": 1.56, "sca": 3.8, "tt2": 1.0, "fix": 60.0, "hop": 120.0, "self": 60.0, "dma": 2200.0, "bpn": 250.0,
+       "rem": 2500.0, "look": 60.0, "rounds": 4000, "seed": 1, "dn": ()}
+GUESS = [dict(), dict(fix=20.0, hop=60.0, self=40.0), dict(fix=100.0, hop=200.0, self=100.0), dict(pe=0.8, tt2=2.0)]
+PERT = {}
+PLAN = {}
+
+NP, NT, NW, NH, WIN = 4096, 1024, 256, 2048, 6400
+SCRATCH = {
+    "ci": ("sbuf", [128, NP], "int32"), "tabc": ("sbuf", [128, WIN], "float32"),
+    "tabr": ("sbuf", [128, WIN], "int32"), "tabb": ("sbuf", [128, WIN], "bfloat16"),
+    "bf": ("sbuf", [128, 28672], "bfloat16"), "hf": ("sbuf", [128, 6144], "float16"), "ff": ("sbuf", [128, 8192], "float32"),
+    "ii": ("sbuf", [128, 2560], "int32"), "uu": ("sbuf", [128, 512], "uint16"), "eq": ("sbuf", [128, 16, 256], "bfloat16"),
+}
+for _k in range(8):
+    SCRATCH["p%d" % _k] = ("psum", [128, 512], "float32")
+NLOAD = 8
+SEMAPHORES = ["dve", "act", "pe", "pool", "sent"] + ["d%d" % _k for _k in range(NLOAD + 6)] + ["r%d" % _k for _k in range(4)]
+
+
+def build(g, T, topo, core, dst):
+    ops = []
+    top = {"bf": 0, "hf": 0, "ff": 0, "ii": 0, "uu": 0}
+    named = {}
+    v, s, pe = g.vector, g.scalar, g.tensor
+    cyc, fix = CFG["cyc"], CFG["fix"]
+
+    def view(name, lo, hi, step=1):
+        return (name, lo, hi, T[name][:, lo:hi] if step == 1 else T[name][:, lo:hi:step])
+
+    def new(key, arena, n):
+        if key not in named:
+            lo = top[arena]
+            top[arena] = lo + (n + 15) // 16 * 16
+            assert top[arena] <= SCRATCH[arena][1][1], arena
+            named[key] = view(arena, lo, lo + n)
+        return named[key]
+
+    def sub(x, lo, hi, step=1):
+        return view(x[0], x[1] + lo, x[1] + hi, step)
+
+    def ps(bank, lo, n):
+        return view("p%d" % bank, lo, lo + n)
+
+    def wid(x):
+        return x[2] - x[1]
+
+    def two(*xs):
+        return all(x[0] in ("bf", "hf", "tabb", "uu", "eq") for x in xs)
+
+    def op(eng, cost, fn, reads, writes, **kw):
+        ops.append(dict(eng=eng, cost=cost, fn=fn, reads=[x for x in reads if isinstance(x, tuple)], writes=writes, **kw))
+
+    def ap(x):
+        return x[3] if isinstance(x, tuple) else x
+
+    def ind(win, off):
+        return win[3].indirect(off[3])
+
+    def act(out, in_, func, bias=0.0, scale=1.0, off=None):
+        op("act", fix + max(64, wid(out) * (CFG["gat"] if off else 1.0)) * cyc,
+           lambda: s.activation(out[3], ind(in_, off) if off else in_[3], func, bias=ap(bias), scale=ap(scale)), [in_, bias, scale, off], [out])
+
+    def ts(out, in_, s1, o1, s2=None, o2=None):
+        c = fix + max(64, wid(out) * (0.5 if two(out, in_) else 1.0)) * cyc
+        if o2 is None:
+            op("dve", c, lambda: v.tensor_scalar(out[3], in_[3], ap(s1), None, o1), [in_, s1], [out])
+        else:
+            op("dve", c, lambda: v.tensor_scalar(out[3], in_[3], ap(s1), ap(s2), o1, o2), [in_, s1, s2], [out])
+
+    def cp(out, in_, soff=None):
+        k = CFG["sca"] if soff else 0.5 if two(out, in_) else 1.0
+        op("dve", fix + max(64, wid(in_) * k) * cyc, lambda: v.tensor_copy(ind(out, soff) if soff else out[3], in_[3]), [in_, soff], [out])
+
+    def tt(out, a, b, o, off=None, soff=None):
+        if off:
+            k = CFG["gat"]
+        elif soff:
+            k = CFG["sca"]
+        elif a[0][0] == "p" or b[0][0] == "p":
+            k = 1.0
+        else:
+            k = CFG["tt2"] if two(out, a, b) else 2.0
+        op("dve", fix + max(64, wid(b) * k) * cyc,
+           lambda: v.tensor_tensor(ind(out, soff) if soff else out[3], ind(a, off) if off else a[3], b[3], o), [a, b, off, soff], [out])
+
+    def mm(out, terms, start=True, stop=True):
+        c = sum(max(64, wid(out)) for w, r in terms) * CFG["pe"] + 30
+
+        def fn():
+            last = None
+            for k, (w, r) in enumerate(terms):
+                last = pe.matmul(out[3], w[3], r[3], start and k == 0, stop and k == len(terms) - 1)
+            return last
+        op("pe", c, fn, [x for t in terms for x in t] + ([] if start else [out]), [out])
+
+    def compact(out, z, src, extra=()):
+        mm(out, list(extra) + [(sub(z, 15 - i, 143 - i), sub(src, i, wid(src), 16)) for i in range(16)])
+
+    def sel(out, in_, pattern, cmp, base, mult, fill=0.0):
+        op("pool", 170 + 2 * wid(out) * cyc, lambda: g.affine_select(out[3], in_[3], pattern, cmp, fill, base, mult), [in_], [out])
+
+    def fill(out, c):
+        op("dve", fix + max(64, wid(out) * 0.5) * cyc, lambda: v.memset(out[3], c), [], [out])
+
+    nd, nr = [0], [0]
+
+    def dma(out, in_, nbytes, reads, writes):
+        sem = T.sem["d%d" % nd[0]]
+        nd[0] += 1
+        op("sync", 60, lambda: g.sync.dma_start(out, in_).then_inc(sem, 16), reads, writes, sem=sem, val=16, nbytes=nbytes)
+
+    rid, pid, _se = topo.addr(dst)
+    mask = topo.mask(core, dst)
+    neng = len(topo.engines(core, dst))
+
+    def send(land, srcs):
+        sem = T.sem["r%d" % nr[0]]
+        nr[0] += 1
+        if len(srcs) == 1:
+            fn = lambda: g.remote_dma(land[3], srcs[0][3], sem, T.sem.sent, pid, rid, mask)
+        else:
+            fn = lambda: g.remote_dma_fused([RemoteDMATransfer(dst_ids=[DstId(rid=rid, pnc=pid)], dma_engine_mask=mask, remote_sem=sem,
+                                                               srcs=[x[3] for x in srcs], dsts=[land[3]], alu_op=1)], local_sem=T.sem.sent)
+        op("pool", 300, fn, srcs, [land], sem=sem, val=neng, remote=True, nbytes=wid(land) * 256 * len(srcs))
+
+    trav = new("trav", "bf", NT)
+    wi, thi = new("wi", "ii", 1), new("thi", "ii", 1)
+    CH = NP // NLOAD
+    for k in range(NLOAD):
+        c = view("ci", k * CH, (k + 1) * CH)
+        dma(c[3], T.peers[:, k * CH:(k + 1) * CH], CH * 512, [], [c])
+        if k == 0:
+            dma(trav[3], T.trav[:], NT * 256, [], [trav])
+            dma(wi[3], T.wts[:], 512, [], [wi])
+        if k == 2:
+            dma(thi[3], T.th[:], 512, [], [thi])
+
+    def W(key, arena="bf", n=128):
+        return new("W" + key, arena, n)
+    one = W("one", "bf", 256)
+    fill(one, 1.0)
+    o128 = sub(one, 0, 128)
+    sel(W("I"), o128, [[-1, 128]], A.is_equal, 0, 1)
+    sel(W("b0"), o128, [[-16, 8], [0, 16]], A.is_ge, 0, 1)
+    sel(W("Blk"), W("b0"), [[16, 8], [0, 16]], A.is_ge, 15, -1)
+    sel(W("L"), W("Blk"), [[1, 128]], A.is_gt, 0, -1)
+    sel(W("U"), W("Blk"), [[-1, 128]], A.is_gt, 0, 1)
+    h0, h1, h2, thr = (W(key, "bf", 256) for key in ("h0", "h1", "h2", "thr"))
+    sel(h0, one, [[0, 16], [1, 16]], A.is_gt, 0, 0)
+    ts(h1, h0, -2.0, A.mult, 2.0, A.add)
+    ts(h2, h0, 0.5, A.mult)
+    op("dve", fix + 128 * cyc, lambda: v.tensor_tensor_scan(thr[3], h2[3], h1[3], 0.0, A.mult, A.add), [h2, h1], [thr])
+    Z = W("Z", "bf", 144)
+    fill(Z, 0.0)
+    op("dve", fix + 64 * cyc, lambda: v.tensor_copy(sub(Z, 15, 143, 16)[3], sub(W("Blk"), 0, 128, 16)[3]), [W("Blk"), Z], [Z])
+    for key, src, c in (("nI", "I", -1.0), ("n2I", "I", -2.0), ("nhI", "I", -0.5), ("hI", "I", 0.5), ("I256", "I", 256.0), ("L4", "L", 4.0),
+                        ("Blk64", "Blk", 64.0), ("BlkS", "Blk", 1.0 / 2048), ("U16", "U", 16.0)):
+        act(W(key), W(src), F.Copy, scale=c)
+    for key, src, c in (("Blkh", "Blk", 1.0), ("I64h", "I", 64.0), ("nI64h", "I", -64.0)):
+        ts(W(key, "hf"), W(src), c, A.mult)
+    tt(W("Wval"), W("I"), W("L4"), A.subtract)
+    tt(W("WX"), W("I"), W("L4"), A.add)
+    act(W("nWX"), W("WX"), F.Copy, scale=-1.0)
+    Zh, Z256, Zw = W("Zh", "hf", 144), W("Z256", "bf", 144), W("Zw", "bf", 144)
+    cp(Zh, Z)
+    act(Z256, Z, F.Copy, scale=256.0)
+    col = lambda key: new("c" + key, "ff", 1)
+    tt(W("tmp"), W("I"), sub(thr, 0, 128), A.mult)
+    op("dve", fix + 128 * cyc, lambda: v.tensor_reduce(col("p2")[3], W("tmp")[3], AX.X, A.add), [W("tmp")], [col("p2")])
+    op("dve", fix + 128 * cyc, lambda: v.tensor_reduce(col("lev")[3], W("U")[3], AX.X, A.add), [W("U")], [col("lev")])
+    ts(W("Wd"), W("Blk"), col("p2"), A.mult, 0.5, A.mult)
+    act(col("last"), col("lev"), F.Sigmoid, bias=-14.5 * 256, scale=256.0)
+    ts(col("at"), col("last"), 256.0, A.mult, -128.0, A.add)
+    j16, jc = new("j16", "ff", 16), new("jc", "bf", 16)
+    op("pool", 160, lambda: g.iota(j16[3], [[16, 16]], 0, 0, allow_small_or_imprecise_dtypes=True), [], [j16])
+    ts(jc, j16, col("lev"), A.add)
+    ts(col("w"), wi, 0.25, A.mult)
+    ts(col("k"), thi, -256.0, A.mult, -64.0 * 7166, A.add)
+    act(Zw, Z, F.Identity, scale=col("w"))
+    act(W("Blkw"), W("Blk"), F.Identity, scale=col("w"))
+    I, nI, n2I, WX, I256 = W("I"), W("nI"), W("n2I"), W("WX"), W("I256")
+
+    NN = NT - NW
+    parts = [(0, NN // 2), (NN // 2, NN)]
+    st = new("st0", "bf", 2 * NW)
+    xN, DN = new("xN0", "bf", NN), new("DN0", "bf", NN)
+    xN1, DN1, st3 = new("xN1", "bf", NN), new("DN1", "bf", NN), new("st3", "bf", 2 * NW)
+    tmp = new("tmpT", "bf", NT)
+    pieces = [(sub(trav, 0, NW), sub(st, 0, NW), sub(st, NW, 2 * NW), sub(tmp, 0, NW), 3)]
+    pieces += [(sub(trav, NW + a, NW + b), sub(xN, a, b), sub(DN, a, b), sub(tmp, NW + a, NW + b), k) for k, (a, b) in enumerate(parts)]
+    for sv, xv, dv, tv, bank in pieces:
+        act(tv, sv, F.Identity, bias=191.75, scale=0.25)
+        act(dv, tv, F.Identity, bias=-768.0, scale=4.0)
+        pa = ps(bank, 0, wid(sv))
+        mm(pa, [(I, sv), (nI, dv)])
+        act(tv, pa, F.Abs, bias=-2.5, scale=2.0)
+        ts(xv, tv, -1.0, A.mult, 1.5, A.add)
+    send(DN1, [DN])
+
+    def offs(t):
+        return new("off%d" % t, "uu", 64)
+
+    def first(t, dv, p, lo, hi):
+        compact(p, Zw, dv)
+        a, b = new("fa%d" % lo, "ii", hi - lo), new("fb%d" % lo, "ii", hi - lo)
+        cp(a, p)
+        ts(b, a, NP - 1, A.bitwise_and)
+        cp(sub(offs(t), lo, hi), b)
+        return b
+
+    def first_w(t, dv):
+        ts(new("mcf%d" % t, "ff", 16), first(t, dv, ps(2, 448, 16), 0, 16), -2048.0, A.add)
+        p = ps(7, 256, NW)
+        mm(p, [(W("Blkw"), dv)])
+        a, b = new("fw3", "ii", NW), new("fw4", "ii", NW)
+        cp(a, p)
+        ts(b, a, NP - 1, A.bitwise_and)
+        ts(new("M%d" % t, "hf", NW), b, -2048.0, A.add)
+
+    first_w(0, sub(st, NW, 2 * NW))
+    first(0, DN, ps(2, 400, 48), 16, 64)
+
+    for k in range(NLOAD):
+        lo, hi = k * CH, (k + 1) * CH
+        c = view("ci", lo, hi)
+        bi = new("bi%d" % (k % 2), "ii", CH)
+        act(view("tabc", lo, hi), c, F.Copy)
+        ts(bi, c, 3, A.bitwise_and)
+        act(view("tabb", lo, hi), bi, F.Copy)
+        ts(view("tabr", lo, hi), c, -31.0 - 64 * 2048, A.add, 1.0 / 64, A.mult)
+    gB, gR, gC = view("tabb", 0, NP), view("tabr", 0, NP), view("tabc", 0, NP)
+    sB, sR, sC = view("tabb", 0, WIN), view("tabr", 0, WIN), view("tabc", 0, WIN)
+    out = new("out", "bf", NT)
+    SIG = (1.0 + 2.0 ** -18) / 64
+    BIG = 2.0 ** 23
+
+    def finish(xs, ds, lo, bank):
+        n = wid(xs[0])
+        y0, p = sub(tmp, lo, lo + n), ps(bank, 0, n)
+        if len(xs) > 1:
+            mm(p, [(I, u) for u in xs])
+        act(y0, p if len(xs) > 1 else xs[0], F.Abs, bias=0.5, scale=-2.0)
+        mm(p, [(I, u) for u in ds] + [(nI, y0)])
+        act(sub(out, lo, lo + n), p, F.Identity, bias=2.5)
+
+    for t in range(6):
+        ph, par = t % 3, t % 2
+        B = lambda key, arena="bf", n=NW: new("%s%d" % (key, par), arena, n)
+        if t == 3:
+            first(3, DN1, ps(2, 400, 48), 16, 64)
+            st, xN, DN = st3, xN1, DN1
+            first_w(3, sub(st, NW, 2 * NW))
+        x, D4 = sub(st, 0, NW), sub(st, NW, 2 * NW)
+        ch = new("ch%d" % (t == 2), "bf", 2 * NW)
+        dx, y = sub(ch, 0, NW), sub(ch, NW, 2 * NW)
+        off, M, mcf = offs(t), new("M%d" % t, "hf", NW), new("mcf%d" % t, "ff", 16)
+        oW = sub(off, 0, 16)
+        b, q = B("b"), B("q")
+        act(b, gB, F.Copy, off=oW)
+        p = ps(3, 0, NW)
+        mm(p, [(I, x), (I, b)])
+        act(q, p, F.Abs, bias=-2.0)
+        pv = ps(4, 0, NW)
+        if ph < 2:
+            mm(pv, [(W("Wval"), q)])
+            act(B("at"), pv, F.Sigmoid, bias=col("at"), scale=256.0)
+            z = B("z", "hf")
+            tt(z, gR, B("at"), A.mult, off=oW)
+            p = ps(2, 448, 16)
+            compact(p, Zh, z)
+            ts(sub(offs(t + 1), 0, 16), p, 2048.0, A.add)
+            cp(new("mcf%d" % (t + 1), "ff", 16), p)
+            p = ps(7, 256, NW)
+            mm(p, [(W("Blkh", "hf"), z)])
+            cp(new("M%d" % (t + 1), "hf", NW), p)
+        cr, tq, r64 = B("cr", "ff"), B("tq", "ff"), B("r64", "ff")
+        act(cr, gC, F.Copy, off=oW)
+        if ph < 2:
+            act(r64, gR, F.Relu, bias=64.0 * 2048, scale=64.0, off=oW)
+        else:
+            act(tq, cr, F.Identity, bias=BIG - 0.5, scale=SIG)
+            act(r64, tq, F.Relu, bias=-64 * BIG, scale=64.0)
+        tt(B("s"), gC, r64, A.subtract, off=oW)
+        pu = ps(6, 0, NW)
+        mm(pu, [(I, B("s")), (nI, b), (nI, D4)])
+        act(B("au"), pu, F.Abs)
+        act(B("ru"), pu, F.Relu)
+        pc = ps(5, 0, NW)
+        mm(pc, [(nI, thr)], True, False)
+        for c in range(16):
+            n = NW - 16 * c
+            e = ("eq", c * 256, c * 256 + n, T.eq[:, c, 0:n])
+            ts(e, sub(M, 16 * c, NW), sub(mcf, c, c + 1), A.is_equal)
+            if c < 15:
+                mm(sub(pc, 16 * c + 16, NW), [(W("Blk64"), ("eq", c * 256 + 16, c * 256 + n, T.eq[:, c, 16:n]))], False, False)
+        mm(pc, [(W("Wd"), ("eq", 0, 4096, T.eq[:, :, 0:16]))], False, True)
+        tw = B("tw")
+        act(tw, pc, F.Sign, bias=2.0 ** -16)
+        pk = ps(4, 256, NW)
+        mm(pk, [(W("Wval"), q), (W("BlkS"), B("au")), (W("nhI"), tw)])
+        k1 = B("k1")
+        act(k1, pk, F.Sigmoid, bias=col("k"), scale=131072.0)
+        p = ps(3, 256, NW)
+        mm(p, [(WX, q), (I256, x), (n2I, k1)])
+        act(dx, p, F.Relu, bias=-253.0, scale=-1.0)
+        p = ps(6, 256, NW)
+        mm(p, [(I, B("ru")), (W("Blk64"), k1)])
+        act(y, p, F.Relu, bias=-64.0)
+        if t == 2:
+            send(st3, [st, ch])
+        p = ps(3, 0, NW)
+        mm(p, [(WX, q), (I256, b), (n2I, k1)])
+        act(B("db"), p, F.Relu, bias=3.0, scale=-1.0)
+        p = ps(2, 464, 16)
+        compact(p, Z256, tw, [(I, jc)])
+        tt(B("o2", "ff", 16), p, mcf, A.max)
+        o2 = B("off2", "uu", 16)
+        ts(o2, B("o2", "ff", 16), 2048.0, A.add)
+        kap = new("kap%d" % ph, "bf", NW)
+        if ph < 2:
+            act(kap, dx, F.Sign)
+        dl = B("dl", "ff")
+        if ph == 0:
+            p = ps(3, 256, NW)
+            mm(p, [(I, B("db")), (nI, y)])
+            act(dl, p, F.Copy)
+        else:
+            p = ps(7, 0, NW)
+            mm(p, [(WX, q), (W("hI"), x), (W("nhI"), b), (I256, tw)])
+            act(B("k5"), p, F.Abs, bias=255.5)
+            act(B("k4"), B("k5"), F.Relu, bias=1.0, scale=-2.0)
+            held = [(I256, new("kap%d" % k, "bf", NW)) for k in range(ph)]
+            mm(pv, held + [(W("Wval"), q), (n2I, b), (W("U16"), B("k4"))])
+            act(B("mu"), pv, F.Sigmoid, bias=-256.0 * 256, scale=256.0)
+            r16 = B("r16", "hf")
+            ts(r16, r64, 1.0 / 64, A.mult, -2048.0, A.add)
+            M1 = new("M%d" % (t - ph), "hf", NW)
+            p1, p2, p3 = (new(u, "hf", NW) for u in ("pp1", "pp2", "pp3"))
+            pu = ps(7, 256, NW)
+            mm(pu, [(W("I64h", "hf"), u) for u in ([M1] if ph == 1 else [p1, p2, p3])] + [(W("nI64h", "hf"), r16)])
+            dr = B("dr", "ff")
+            tt(dr, pu, B("mu"), A.mult)
+            p = ps(3, 256, NW)
+            mm(p, [(I, B("db")), (nI, y)])
+            tt(dl, p, dr, A.add)
+            if ph == 1:
+                act(B("nu"), pv, F.Sigmoid, bias=-262.0 * 256, scale=256.0)
+                tt(p1, r16, B("nu"), A.mult)
+                tt(B("om"), new("kap0", "bf", NW), B("nu"), A.subtract)
+                tt(p3, M1, B("om"), A.mult)
+                tt(p2, M, kap, A.mult)
+        if ph < 2:
+            stn = new("sn%d" % t, "bf", 2 * NW)
+            tt(sub(stn, 0, NW), x, dx, A.add)
+            tt(sub(stn, NW, 2 * NW), D4, y, A.add)
+            st = stn
+        zN = B("zN", "hf", NN)
+        for k, (lo, hi) in enumerate(parts):
+            n = hi - lo
+            oN, xv = sub(off, 16 + lo // 16, 16 + hi // 16), sub(xN, lo, hi)
+            bN, qN = (sub(B(key, "bf", NN), lo, hi) for key in ("bN", "qN"))
+            p = ps(k, 0, n)
+            if (t, k) in CFG["dn"]:
+                tt(bN, gB, xv, A.add, off=oN)
+                act(qN, bN, F.Abs, bias=-2.0)
+            else:
+                act(bN, gB, F.Copy, off=oN)
+                mm(p, [(I, xv), (I, bN)])
+                act(qN, p, F.Abs, bias=-2.0)
+            if ph < 2:
+                aN, pv2 = sub(B("aN", "bf", NN), lo, hi), ps(2, 0, n)
+                mm(pv2, [(W("Wval"), qN)])
+                act(aN, pv2, F.Sigmoid, bias=col("at"), scale=256.0)
+                tt(sub(zN, lo, hi), gR, aN, A.mult, off=oN)
+            mm(p, [(W("nWX"), qN), (n2I, xv)])
+            tt(xv, p, xv, A.max)
+            if t == 2:
+                send(sub(xN1, lo, hi), [xv])
+            if t == 5:
+                finish([xv], [sub(DN, lo, hi)], NW + lo, k)
+        if ph < 2:
+            p = ps(2, 400, 48)
+            compact(p, Zh, zN)
+            ts(sub(offs(t + 1), 16, 64), p, 2048.0, A.add)
+        if t < 5:
+            tt(sB, b, B("db"), A.add, soff=o2)
+        tt(sC, cr, dl, A.add, soff=o2)
+        if t in (1, 2):
+            tt(B("rf", "ff"), r64, B("dr", "ff"), A.add)
+            act(B("rn", "ff"), B("rf", "ff"), F.Identity, bias=-2048.0, scale=1.0 / 64)
+            cp(sR, B("rn", "ff"), soff=o2)
+    yp = view("tabc", 0, NH)
+    dma(T.yp[:], yp[3], NH * 512, [yp], [])
+    finish([x, dx], [D4, y], 0, 3)
+    dma(T.yt[:, 0:NW], sub(out, 0, NW)[3], NW * 256, [sub(out, 0, NW)], [])
+    dma(T.yt[:, NW:NT], sub(out, NW, NT)[3], NN * 256, [sub(out, NW, NT)], [])
+    return ops, nr[0] * neng
+
+
+def links(ops):
+    deps = [set() for _ in ops]
+    seen = {}
+    for i, o in enumerate(ops):
+        for kind, lst in (("r", o["reads"]), ("w", o["writes"])):
+            for x in lst:
+                for (j, k2, lo, hi) in seen.get(x[0], []):
+                    if j != i and lo < x[2] and x[1] < hi and (kind == "w" or k2 == "w"):
+                        deps[i].add(j)
+        for kind, lst in (("r", o["reads"]), ("w", o["writes"])):
+            for x in lst:
+                rest = seen.get(x[0], [])
+                if kind == "w":
+                    rest = [e for e in rest if not (x[1] <= e[2] and e[3] <= x[2])]
+                seen[x[0]] = rest + [(i, kind, x[1], x[2])]
+    return deps
+
+
+def plan(ops, base=None):
+    n = len(ops)
+    deps = [set(d) for d in (base or links(ops))]
+    lat = [0.0 if "nbytes" not in o else (CFG["rem"] if o.get("remote") else CFG["dma"]) for o in ops]
+    succ = [[] for _ in range(n)]
+    for i in range(n):
+        for j in deps[i]:
+            succ[j].append(i)
+    prio = [0.0] * n
+    for i in range(n - 1, -1, -1):
+        prio[i] = ops[i]["cost"] + lat[i] + ops[i].get("nbytes", 0) / CFG["bpn"] + max([prio[k] + CFG["hop"] for k in succ[i]] + [0.0])
+    for i in range(n):
+        prio[i] += PERT.get(i, 0.0) + (1e6 - i if ops[i]["eng"] == "sync" and not ops[i]["reads"] else 0.0)
+    eng = [o["eng"] for o in ops]
+    banks = [sorted(set(x[0] for x in o["reads"] + o["writes"] if x[0][0] == "p")) for o in ops]
+    free, done, left = {}, [0.0] * n, [len(d) for d in deps]
+    user, order, wire, since = {}, [], 0.0, [0.0] * n
+    ready = [i for i in range(n) if left[i] == 0]
+    while ready:
+        es = []
+        for i in ready:
+            t = max(free.get(eng[i], 0.0), since[i])
+            for bk in banks[i]:
+                for u in user.get(bk, {}).values():
+                    if eng[u] != eng[i]:
+                        t = max(t, done[u] + CFG["hop"])
+            es.append((t, i))
+        t0, i0 = min(es)
+        t, i = max([e for e in es if eng[e[1]] == eng[i0] and e[0] <= t0 + CFG["look"]], key=lambda e: prio[e[1]])
+        o = ops[i]
+        for bk in banks[i]:
+            for u in user.get(bk, {}).values():
+                if eng[u] != eng[i]:
+                    deps[i].add(u)
+            user.setdefault(bk, {})[eng[i]] = i
+        free[eng[i]] = done[i] = t + o["cost"]
+        if "nbytes" in o:
+            wire = max(wire, done[i] + lat[i]) + o["nbytes"] / CFG["bpn"]
+            done[i] = wire
+        order.append((i, t, done[i]))
+        ready.remove(i)
+        for k in succ[i]:
+            if not (eng[k] == "pe" and eng[i] == "pe"):
+                since[k] = max(since[k], done[i] + (CFG["self"] if eng[k] == eng[i] else CFG["hop"]))
+            left[k] -= 1
+            if left[k] == 0:
+                ready.append(k)
+    return order, deps
+
+
+def replay(ops, order, deps, cfg, cost):
+    free, done, wire = {}, {}, 0.0
+    for i, _t, _d in order:
+        o = ops[i]
+        e = o["eng"]
+        t = free.get(e, 0.0)
+        for j in deps[i]:
+            f = ops[j]["eng"]
+            if f != e:
+                t = max(t, done[j] + cfg["hop"])
+            elif e != "pe":
+                t = max(t, done[j] + cfg["self"])
+        free[e] = done[i] = t + cost[i]
+        if "nbytes" in o:
+            wire = max(wire, done[i] + (cfg["rem"] if o.get("remote") else cfg["dma"])) + o["nbytes"] / cfg["bpn"]
+            done[i] = wire
+    return max(done.values())
+
+
+def shape(make):
+    keep, sets = dict(CFG), []
+    for gs in GUESS:
+        CFG.update(keep)
+        CFG.update(gs)
+        sets.append((dict(CFG), [o["cost"] for o in make()]))
+    CFG.update(keep)
+    ops = make()
+    base, n, seed = links(ops), len(ops), [CFG["seed"]]
+
+    def draw(k):
+        seed[0] = (seed[0] * 1103515245 + 12345) % 2147483648
+        return (seed[0] >> 8) % k
+
+    def total(p):
+        PERT.clear()
+        PERT.update(p)
+        got = plan(ops, base)
+        return sum(replay(ops, got[0], got[1], c, x) for c, x in sets), got
+    pert = {}
+    best, got = total(pert)
+    for _ in range(CFG["rounds"]):
+        p, a = dict(pert), draw(n)
+        for _k in range(1 << draw(3)):
+            j = min(n - 1, max(0, a + draw(61) - 30))
+            p[j] = p.get(j, 0.0) + 100.0 * (draw(21) + draw(21) - 20)
+        r, o = total(p)
+        if r < best - 1.0:
+            best, got, pert = r, o, p
+    PERT.clear()
+    PERT.update(pert)
+    return got
+
+
+def rank_program(g, core, T, topo):
+    rank = T.rank_of(core)
+    if rank is None:
+        return
+    dst = T.cores[(rank + 1) % len(T.cores)]
+    ops, nsent = build(g, T, topo, core, dst)
+    if "p" not in PLAN:
+        PLAN["p"] = shape(lambda: build(g, T, topo, core, dst)[0])
+    order, deps = PLAN["p"]
+    queue = {"dve": g.vector, "act": g.scalar, "pe": g.tensor, "pool": g, "sync": g.sync}
+    count, mark, waited = {}, {}, {}
+    for i, _t, _d in order:
+        o = ops[i]
+        e = o["eng"]
+        need = {}
+        for j in deps[i]:
+            if e == "pe" and ops[j]["eng"] == "pe":
+                continue
+            key, sem, val = mark[j]
+            if val > need.get(key, (None, 0))[1]:
+                need[key] = (sem, val)
+        for key in sorted(need):
+            sem, val = need[key]
+            if waited.get((e, key), 0) < val:
+                queue[e].wait_ge(sem, val)
+                waited[(e, key)] = val
+        ins = o["fn"]()
+        if "sem" in o:
+            mark[i] = ("x%d" % i, o["sem"], o["val"])
+        else:
+            count[e] = count.get(e, 0) + 1
+            ins.then_inc(T.sem[e], 1)
+            mark[i] = (e, T.sem[e], count[e])
+    for e in sorted(count):
+        g.wait_ge(T.sem[e], count[e])
+    g.wait_ge(T.sem.sent, nsent)
+    for o in ops:
+        if "sem" in o:
+            g.wait_ge(o["sem"], o["val"])

@@ -2,22 +2,22 @@ from concourse.bass import DstId, RemoteDMATransfer
 from concourse.mybir import AluOpType as A, ActivationFunctionType as F, AxisListType as AX
 
 CFG = {"cyc": 1.04, "pe": 0.52, "gat": 1.56, "sca": 3.8, "tt2": 1.0, "fix": 60.0, "hop": 120.0, "self": 60.0, "dma": 2200.0, "bpn": 250.0,
-       "rem": 2500.0, "look": 60.0, "rounds": 4000, "seed": 1, "dn": ()}
-GUESS = [dict(), dict(fix=20.0, hop=60.0, self=40.0), dict(fix=100.0, hop=200.0, self=100.0), dict(pe=0.8, tt2=2.0)]
-PERT = {}
+       "rem": 2500.0, "look": 60.0, "rounds": 5500, "seed": 1}
+GUESS = [dict(cyc=0.9, pe=0.45, fix=40.0, hop=100.0, self=50.0), dict(cyc=1.2, pe=0.6, gat=2.05, sca=5.8),
+         dict(bpn=150.0, dma=3000.0, rem=4000.0, hop=250.0), dict(tt2=2.0, gat=1.2, sca=2.5)]
 PLAN = {}
 
 NP, NT, NW, NH, WIN = 4096, 1024, 256, 2048, 6400
 SCRATCH = {
     "ci": ("sbuf", [128, NP], "int32"), "tabc": ("sbuf", [128, WIN], "float32"),
-    "tabr": ("sbuf", [128, WIN], "int32"), "tabb": ("sbuf", [128, WIN], "bfloat16"),
-    "bf": ("sbuf", [128, 28672], "bfloat16"), "hf": ("sbuf", [128, 6144], "float16"), "ff": ("sbuf", [128, 8192], "float32"),
-    "ii": ("sbuf", [128, 2560], "int32"), "uu": ("sbuf", [128, 512], "uint16"), "eq": ("sbuf", [128, 16, 256], "bfloat16"),
+    "tabr": ("sbuf", [128, NP], "int32"), "tabb": ("sbuf", [128, WIN], "int32"),
+    "bf": ("sbuf", [128, 30720], "bfloat16"), "hf": ("sbuf", [128, 6144], "float16"), "ff": ("sbuf", [128, 8192], "float32"),
+    "ii": ("sbuf", [128, 1024], "int32"), "uu": ("sbuf", [128, 512], "uint16"), "eq": ("sbuf", [128, 16, 256], "bfloat16"),
 }
 for _k in range(8):
     SCRATCH["p%d" % _k] = ("psum", [128, 512], "float32")
-NLOAD = 8
-SEMAPHORES = ["dve", "act", "pe", "pool", "sent"] + ["d%d" % _k for _k in range(NLOAD + 6)] + ["r%d" % _k for _k in range(4)]
+CUTS = [0, 512, 1152, 1792, 2432, 2944, 3456, 3840, 4096]
+SEMAPHORES = ["dve", "act", "pe", "pool", "sent"] + ["d%d" % _k for _k in range(14)] + ["r%d" % _k for _k in range(4)]
 
 
 def build(g, T, topo, core, dst):
@@ -48,10 +48,15 @@ def build(g, T, topo, core, dst):
         return x[2] - x[1]
 
     def two(*xs):
-        return all(x[0] in ("bf", "hf", "tabb", "uu", "eq") for x in xs)
+        return all(x[0] in ("bf", "hf", "uu", "eq") for x in xs)
 
     def op(eng, cost, fn, reads, writes, **kw):
-        ops.append(dict(eng=eng, cost=cost, fn=fn, reads=[x for x in reads if isinstance(x, tuple)], writes=writes, **kw))
+        ops.append(dict(ways=[(eng, cost, fn)], reads=[x for x in reads if isinstance(x, tuple)], writes=writes, **kw))
+
+    def both():
+        o = ops.pop()
+        ops[-1]["ways"] += o["ways"]
+        ops[-1]["reads"] += o["reads"]
 
     def ap(x):
         return x[3] if isinstance(x, tuple) else x
@@ -70,9 +75,10 @@ def build(g, T, topo, core, dst):
         else:
             op("dve", c, lambda: v.tensor_scalar(out[3], in_[3], ap(s1), ap(s2), o1, o2), [in_, s1, s2], [out])
 
-    def cp(out, in_, soff=None):
-        k = CFG["sca"] if soff else 0.5 if two(out, in_) else 1.0
-        op("dve", fix + max(64, wid(in_) * k) * cyc, lambda: v.tensor_copy(ind(out, soff) if soff else out[3], in_[3]), [in_, soff], [out])
+    def cp(out, in_, off=None, soff=None):
+        k = CFG["sca"] if soff else CFG["gat"]
+        op("dve", fix + max(64, wid(in_ if soff else out) * k) * cyc,
+           lambda: v.tensor_copy(ind(out, soff) if soff else out[3], ind(in_, off) if off else in_[3]), [in_, off, soff], [out])
 
     def tt(out, a, b, o, off=None, soff=None):
         if off:
@@ -85,6 +91,26 @@ def build(g, T, topo, core, dst):
             k = CFG["tt2"] if two(out, a, b) else 2.0
         op("dve", fix + max(64, wid(b) * k) * cyc,
            lambda: v.tensor_tensor(ind(out, soff) if soff else out[3], ind(a, off) if off else a[3], b[3], o), [a, b, off, soff], [out])
+
+    def aff(out, in_, scale=1.0, bias=0.0):
+        act(out, in_, F.Identity, bias=bias, scale=scale)
+        ts(out, in_, scale, A.mult, bias, A.add)
+        both()
+
+    def relu(out, in_, bias):
+        act(out, in_, F.Relu, bias=bias)
+        ts(out, in_, bias, A.add, 0.0, A.max)
+        both()
+
+    def above(out, in_, scale, bias, k, lim):
+        act(out, in_, F.Sigmoid, bias=bias, scale=scale)
+        ts(out, in_, k, A.mult, lim, A.is_gt)
+        both()
+
+    def pick(out, win, off):
+        act(out, win, F.Copy, off=off)
+        cp(out, win, off=off)
+        both()
 
     def mm(out, terms, start=True, stop=True):
         c = sum(max(64, wid(out)) for w, r in terms) * CFG["pe"] + 30
@@ -107,10 +133,10 @@ def build(g, T, topo, core, dst):
 
     nd, nr = [0], [0]
 
-    def dma(out, in_, nbytes, reads, writes):
+    def dma(out, in_, nbytes, reads, writes, eng="sync"):
         sem = T.sem["d%d" % nd[0]]
         nd[0] += 1
-        op("sync", 60, lambda: g.sync.dma_start(out, in_).then_inc(sem, 16), reads, writes, sem=sem, val=16, nbytes=nbytes)
+        op(eng, 80, lambda: (g.sync if eng == "sync" else s).dma_start(out, in_).then_inc(sem, 16), reads, writes, sem=sem, val=16, nbytes=nbytes)
 
     rid, pid, _se = topo.addr(dst)
     mask = topo.mask(core, dst)
@@ -128,15 +154,14 @@ def build(g, T, topo, core, dst):
 
     trav = new("trav", "bf", NT)
     wi, thi = new("wi", "ii", 1), new("thi", "ii", 1)
-    CH = NP // NLOAD
-    for k in range(NLOAD):
-        c = view("ci", k * CH, (k + 1) * CH)
-        dma(c[3], T.peers[:, k * CH:(k + 1) * CH], CH * 512, [], [c])
+    cuts = list(zip(CUTS, CUTS[1:]))
+    for k, (lo, hi) in enumerate(cuts):
+        c = view("ci", lo, hi)
+        dma(c[3], T.peers[:, lo:hi], (hi - lo) * 512, [], [c])
         if k == 0:
-            dma(trav[3], T.trav[:], NT * 256, [], [trav])
-            dma(wi[3], T.wts[:], 512, [], [wi])
-        if k == 2:
-            dma(thi[3], T.th[:], 512, [], [thi])
+            dma(trav[3], T.trav[:], NT * 256, [], [trav], "act")
+            dma(wi[3], T.wts[:], 512, [], [wi], "act")
+            dma(thi[3], T.th[:], 512, [], [thi], "act")
 
     def W(key, arena="bf", n=128):
         return new("W" + key, arena, n)
@@ -150,37 +175,39 @@ def build(g, T, topo, core, dst):
     sel(W("U"), W("Blk"), [[-1, 128]], A.is_gt, 0, 1)
     h0, h1, h2, thr = (W(key, "bf", 256) for key in ("h0", "h1", "h2", "thr"))
     sel(h0, one, [[0, 16], [1, 16]], A.is_gt, 0, 0)
-    ts(h1, h0, -2.0, A.mult, 2.0, A.add)
-    ts(h2, h0, 0.5, A.mult)
+    aff(h1, h0, -2.0, 2.0)
+    aff(h2, h0, 0.5)
     op("dve", fix + 128 * cyc, lambda: v.tensor_tensor_scan(thr[3], h2[3], h1[3], 0.0, A.mult, A.add), [h2, h1], [thr])
     Z = W("Z", "bf", 144)
     fill(Z, 0.0)
     op("dve", fix + 64 * cyc, lambda: v.tensor_copy(sub(Z, 15, 143, 16)[3], sub(W("Blk"), 0, 128, 16)[3]), [W("Blk"), Z], [Z])
-    for key, src, c in (("nI", "I", -1.0), ("n2I", "I", -2.0), ("nhI", "I", -0.5), ("hI", "I", 0.5), ("I256", "I", 256.0), ("L4", "L", 4.0),
-                        ("Blk64", "Blk", 64.0), ("BlkS", "Blk", 1.0 / 2048), ("U16", "U", 16.0)):
-        act(W(key), W(src), F.Copy, scale=c)
-    for key, src, c in (("Blkh", "Blk", 1.0), ("I64h", "I", 64.0), ("nI64h", "I", -64.0)):
-        ts(W(key, "hf"), W(src), c, A.mult)
-    tt(W("Wval"), W("I"), W("L4"), A.subtract)
-    tt(W("WX"), W("I"), W("L4"), A.add)
-    act(W("nWX"), W("WX"), F.Copy, scale=-1.0)
+    for key, src, c, arena in (("nI", "I", -1.0, "bf"), ("n2I", "I", -2.0, "bf"), ("nhI", "I", -0.5, "bf"), ("hI", "I", 0.5, "bf"),
+                               ("I256", "I", 256.0, "bf"), ("L4", "L", 4.0, "bf"), ("nL4", "L", -4.0, "bf"), ("Blk64", "Blk", 64.0, "bf"),
+                               ("BlkS", "Blk", 1.0 / 2048, "bf"), ("U16", "U", 16.0, "bf"),
+                               ("Blkh", "Blk", 1.0, "hf"), ("I64h", "I", 64.0, "hf"), ("nI64h", "I", -64.0, "hf")):
+        aff(W(key, arena), W(src), c)
+    for key, src, c in (("Wval", "nL4", 1.0), ("WX", "L4", 1.0), ("nWX", "nL4", -1.0)):
+        sel(W(key), W(src), [[-1, 128]], A.not_equal, 0, 1, c)
     Zh, Z256, Zw = W("Zh", "hf", 144), W("Z256", "bf", 144), W("Zw", "bf", 144)
-    cp(Zh, Z)
-    act(Z256, Z, F.Copy, scale=256.0)
+    aff(Zh, Z)
+    aff(Z256, Z, 256.0)
     col = lambda key: new("c" + key, "ff", 1)
     tt(W("tmp"), W("I"), sub(thr, 0, 128), A.mult)
     op("dve", fix + 128 * cyc, lambda: v.tensor_reduce(col("p2")[3], W("tmp")[3], AX.X, A.add), [W("tmp")], [col("p2")])
     op("dve", fix + 128 * cyc, lambda: v.tensor_reduce(col("lev")[3], W("U")[3], AX.X, A.add), [W("U")], [col("lev")])
-    ts(W("Wd"), W("Blk"), col("p2"), A.mult, 0.5, A.mult)
+    aff(col("p1"), col("p2"), 0.5)
+    aff(W("Wd"), W("Blk"), col("p1"))
     act(col("last"), col("lev"), F.Sigmoid, bias=-14.5 * 256, scale=256.0)
-    ts(col("at"), col("last"), 256.0, A.mult, -128.0, A.add)
+    aff(col("at"), col("last"), 256.0, -128.0)
+    aff(col("al"), col("last"), -1.0, 0.5)
     j16, jc = new("j16", "ff", 16), new("jc", "bf", 16)
     op("pool", 160, lambda: g.iota(j16[3], [[16, 16]], 0, 0, allow_small_or_imprecise_dtypes=True), [], [j16])
-    ts(jc, j16, col("lev"), A.add)
-    ts(col("w"), wi, 0.25, A.mult)
-    ts(col("k"), thi, -256.0, A.mult, -64.0 * 7166, A.add)
-    act(Zw, Z, F.Identity, scale=col("w"))
-    act(W("Blkw"), W("Blk"), F.Identity, scale=col("w"))
+    aff(jc, j16, 1.0, col("lev"))
+    aff(col("w"), wi, 0.25)
+    aff(col("k"), thi, -256.0, -64.0 * 7166)
+    aff(col("kl"), thi, 4.0, 7166.0)
+    aff(Zw, Z, col("w"))
+    aff(W("Blkw"), W("Blk"), col("w"))
     I, nI, n2I, WX, I256 = W("I"), W("nI"), W("n2I"), W("WX"), W("I256")
 
     NN = NT - NW
@@ -192,12 +219,12 @@ def build(g, T, topo, core, dst):
     pieces = [(sub(trav, 0, NW), sub(st, 0, NW), sub(st, NW, 2 * NW), sub(tmp, 0, NW), 3)]
     pieces += [(sub(trav, NW + a, NW + b), sub(xN, a, b), sub(DN, a, b), sub(tmp, NW + a, NW + b), k) for k, (a, b) in enumerate(parts)]
     for sv, xv, dv, tv, bank in pieces:
-        act(tv, sv, F.Identity, bias=191.75, scale=0.25)
-        act(dv, tv, F.Identity, bias=-768.0, scale=4.0)
+        aff(tv, sv, 0.25, 191.75)
+        aff(dv, tv, 4.0, -768.0)
         pa = ps(bank, 0, wid(sv))
         mm(pa, [(I, sv), (nI, dv)])
         act(tv, pa, F.Abs, bias=-2.5, scale=2.0)
-        ts(xv, tv, -1.0, A.mult, 1.5, A.add)
+        aff(xv, tv, -1.0, 1.5)
     send(DN1, [DN])
 
     def offs(t):
@@ -206,36 +233,31 @@ def build(g, T, topo, core, dst):
     def first(t, dv, p, lo, hi):
         compact(p, Zw, dv)
         a, b = new("fa%d" % lo, "ii", hi - lo), new("fb%d" % lo, "ii", hi - lo)
-        cp(a, p)
+        aff(a, p)
         ts(b, a, NP - 1, A.bitwise_and)
-        cp(sub(offs(t), lo, hi), b)
+        aff(sub(offs(t), lo, hi), b)
         return b
 
     def first_w(t, dv):
-        ts(new("mcf%d" % t, "ff", 16), first(t, dv, ps(2, 448, 16), 0, 16), -2048.0, A.add)
+        aff(new("mcf%d" % t, "ff", 16), first(t, dv, ps(2, 448, 16), 0, 16), 1.0, -2048.0)
         p = ps(7, 256, NW)
         mm(p, [(W("Blkw"), dv)])
         a, b = new("fw3", "ii", NW), new("fw4", "ii", NW)
-        cp(a, p)
+        aff(a, p)
         ts(b, a, NP - 1, A.bitwise_and)
-        ts(new("M%d" % t, "hf", NW), b, -2048.0, A.add)
+        aff(new("M%d" % t, "hf", NW), b, 1.0, -2048.0)
 
     first_w(0, sub(st, NW, 2 * NW))
     first(0, DN, ps(2, 400, 48), 16, 64)
 
-    for k in range(NLOAD):
-        lo, hi = k * CH, (k + 1) * CH
+    for lo, hi in cuts:
         c = view("ci", lo, hi)
-        bi = new("bi%d" % (k % 2), "ii", CH)
-        act(view("tabc", lo, hi), c, F.Copy)
-        ts(bi, c, 3, A.bitwise_and)
-        act(view("tabb", lo, hi), bi, F.Copy)
-        ts(view("tabr", lo, hi), c, -31.0 - 64 * 2048, A.add, 1.0 / 64, A.mult)
+        aff(view("tabc", lo, hi), c)
+        ts(view("tabb", lo, hi), c, 3, A.bitwise_and)
+        aff(view("tabr", lo, hi), c, 1.0 / 64, -31.0 / 64 - 2048)
     gB, gR, gC = view("tabb", 0, NP), view("tabr", 0, NP), view("tabc", 0, NP)
-    sB, sR, sC = view("tabb", 0, WIN), view("tabr", 0, WIN), view("tabc", 0, WIN)
+    sB, sC = view("tabb", 0, WIN), view("tabc", 0, WIN)
     out = new("out", "bf", NT)
-    SIG = (1.0 + 2.0 ** -18) / 64
-    BIG = 2.0 ** 23
 
     def finish(xs, ds, lo, bank):
         n = wid(xs[0])
@@ -244,7 +266,7 @@ def build(g, T, topo, core, dst):
             mm(p, [(I, u) for u in xs])
         act(y0, p if len(xs) > 1 else xs[0], F.Abs, bias=0.5, scale=-2.0)
         mm(p, [(I, u) for u in ds] + [(nI, y0)])
-        act(sub(out, lo, lo + n), p, F.Identity, bias=2.5)
+        aff(sub(out, lo, lo + n), p, 1.0, 2.5)
 
     for t in range(6):
         ph, par = t % 3, t % 2
@@ -252,42 +274,50 @@ def build(g, T, topo, core, dst):
         if t == 3:
             first(3, DN1, ps(2, 400, 48), 16, 64)
             st, xN, DN = st3, xN1, DN1
-            first_w(3, sub(st, NW, 2 * NW))
+            first_w(3, sub(st3, NW, 2 * NW))
         x, D4 = sub(st, 0, NW), sub(st, NW, 2 * NW)
-        ch = new("ch%d" % (t == 2), "bf", 2 * NW)
+        ch = new("ch%d" % t, "bf", 2 * NW)
         dx, y = sub(ch, 0, NW), sub(ch, NW, 2 * NW)
         off, M, mcf = offs(t), new("M%d" % t, "hf", NW), new("mcf%d" % t, "ff", 16)
         oW = sub(off, 0, 16)
         b, q = B("b"), B("q")
-        act(b, gB, F.Copy, off=oW)
+        pick(b, gB, oW)
         p = ps(3, 0, NW)
         mm(p, [(I, x), (I, b)])
         act(q, p, F.Abs, bias=-2.0)
         pv = ps(4, 0, NW)
+        cr, r64, r16 = B("cr", "ff"), B("r64", "ff"), B("r16", "hf")
+        pick(cr, gC, oW)
+        if t in (0, 1, 4):
+            act(r64, gR, F.Identity, bias=64.0 * 2048, scale=64.0, off=oW)
+            rs = (r64, 1.0 / 64, -2048.0)
+        else:
+            ri = new("ri", "ii", NW)
+            aff(ri, cr, 1.0 / 64, -31.0 / 64)
+            aff(r64, ri, 64.0)
+            rs = (ri, 1.0, -2048.0)
+        if t:
+            aff(r16, *rs)
         if ph < 2:
             mm(pv, [(W("Wval"), q)])
-            act(B("at"), pv, F.Sigmoid, bias=col("at"), scale=256.0)
+            above(B("at"), pv, 256.0, col("at"), 1.0, col("al"))
             z = B("z", "hf")
-            tt(z, gR, B("at"), A.mult, off=oW)
+            if t:
+                tt(z, r16, B("at"), A.mult)
+            else:
+                tt(z, gR, B("at"), A.mult, off=oW)
             p = ps(2, 448, 16)
             compact(p, Zh, z)
-            ts(sub(offs(t + 1), 0, 16), p, 2048.0, A.add)
-            cp(new("mcf%d" % (t + 1), "ff", 16), p)
+            aff(sub(offs(t + 1), 0, 16), p, 1.0, 2048.0)
+            aff(new("mcf%d" % (t + 1), "ff", 16), p)
             p = ps(7, 256, NW)
             mm(p, [(W("Blkh", "hf"), z)])
-            cp(new("M%d" % (t + 1), "hf", NW), p)
-        cr, tq, r64 = B("cr", "ff"), B("tq", "ff"), B("r64", "ff")
-        act(cr, gC, F.Copy, off=oW)
-        if ph < 2:
-            act(r64, gR, F.Relu, bias=64.0 * 2048, scale=64.0, off=oW)
-        else:
-            act(tq, cr, F.Identity, bias=BIG - 0.5, scale=SIG)
-            act(r64, tq, F.Relu, bias=-64 * BIG, scale=64.0)
+            aff(new("M%d" % (t + 1), "hf", NW), p)
         tt(B("s"), gC, r64, A.subtract, off=oW)
         pu = ps(6, 0, NW)
-        mm(pu, [(I, B("s")), (nI, b), (nI, D4)])
+        mm(pu, [(nI, D4), (nI, b), (I, B("s"))])
         act(B("au"), pu, F.Abs)
-        act(B("ru"), pu, F.Relu)
+        relu(B("ru"), pu, 0.0)
         pc = ps(5, 0, NW)
         mm(pc, [(nI, thr)], True, False)
         for c in range(16):
@@ -302,13 +332,13 @@ def build(g, T, topo, core, dst):
         pk = ps(4, 256, NW)
         mm(pk, [(W("Wval"), q), (W("BlkS"), B("au")), (W("nhI"), tw)])
         k1 = B("k1")
-        act(k1, pk, F.Sigmoid, bias=col("k"), scale=131072.0)
+        above(k1, pk, 131072.0, col("k"), 2048.0, col("kl"))
         p = ps(3, 256, NW)
         mm(p, [(WX, q), (I256, x), (n2I, k1)])
         act(dx, p, F.Relu, bias=-253.0, scale=-1.0)
         p = ps(6, 256, NW)
         mm(p, [(I, B("ru")), (W("Blk64"), k1)])
-        act(y, p, F.Relu, bias=-64.0)
+        relu(y, p, -64.0)
         if t == 2:
             send(st3, [st, ch])
         p = ps(3, 0, NW)
@@ -318,25 +348,24 @@ def build(g, T, topo, core, dst):
         compact(p, Z256, tw, [(I, jc)])
         tt(B("o2", "ff", 16), p, mcf, A.max)
         o2 = B("off2", "uu", 16)
-        ts(o2, B("o2", "ff", 16), 2048.0, A.add)
+        aff(o2, B("o2", "ff", 16), 1.0, 2048.0)
         kap = new("kap%d" % ph, "bf", NW)
         if ph < 2:
             act(kap, dx, F.Sign)
+            ts(kap, dx, 0.5, A.is_gt)
+            both()
         dl = B("dl", "ff")
         if ph == 0:
             p = ps(3, 256, NW)
             mm(p, [(I, B("db")), (nI, y)])
-            act(dl, p, F.Copy)
+            aff(dl, p)
         else:
             p = ps(7, 0, NW)
             mm(p, [(WX, q), (W("hI"), x), (W("nhI"), b), (I256, tw)])
-            act(B("k5"), p, F.Abs, bias=255.5)
-            act(B("k4"), B("k5"), F.Relu, bias=1.0, scale=-2.0)
+            ts(B("k4"), p, -255.5, A.is_equal)
             held = [(I256, new("kap%d" % k, "bf", NW)) for k in range(ph)]
             mm(pv, held + [(W("Wval"), q), (n2I, b), (W("U16"), B("k4"))])
-            act(B("mu"), pv, F.Sigmoid, bias=-256.0 * 256, scale=256.0)
-            r16 = B("r16", "hf")
-            ts(r16, r64, 1.0 / 64, A.mult, -2048.0, A.add)
+            above(B("mu"), pv, 256.0, -256.0 * 256, 1.0, 256.0)
             M1 = new("M%d" % (t - ph), "hf", NW)
             p1, p2, p3 = (new(u, "hf", NW) for u in ("pp1", "pp2", "pp3"))
             pu = ps(7, 256, NW)
@@ -347,7 +376,7 @@ def build(g, T, topo, core, dst):
             mm(p, [(I, B("db")), (nI, y)])
             tt(dl, p, dr, A.add)
             if ph == 1:
-                act(B("nu"), pv, F.Sigmoid, bias=-262.0 * 256, scale=256.0)
+                above(B("nu"), pv, 256.0, -262.0 * 256, 1.0, 262.0)
                 tt(p1, r16, B("nu"), A.mult)
                 tt(B("om"), new("kap0", "bf", NW), B("nu"), A.subtract)
                 tt(p3, M1, B("om"), A.mult)
@@ -363,17 +392,13 @@ def build(g, T, topo, core, dst):
             oN, xv = sub(off, 16 + lo // 16, 16 + hi // 16), sub(xN, lo, hi)
             bN, qN = (sub(B(key, "bf", NN), lo, hi) for key in ("bN", "qN"))
             p = ps(k, 0, n)
-            if (t, k) in CFG["dn"]:
-                tt(bN, gB, xv, A.add, off=oN)
-                act(qN, bN, F.Abs, bias=-2.0)
-            else:
-                act(bN, gB, F.Copy, off=oN)
-                mm(p, [(I, xv), (I, bN)])
-                act(qN, p, F.Abs, bias=-2.0)
+            pick(bN, gB, oN)
+            mm(p, [(I, xv), (I, bN)])
+            act(qN, p, F.Abs, bias=-2.0)
             if ph < 2:
                 aN, pv2 = sub(B("aN", "bf", NN), lo, hi), ps(2, 0, n)
                 mm(pv2, [(W("Wval"), qN)])
-                act(aN, pv2, F.Sigmoid, bias=col("at"), scale=256.0)
+                above(aN, pv2, 256.0, col("at"), 1.0, col("al"))
                 tt(sub(zN, lo, hi), gR, aN, A.mult, off=oN)
             mm(p, [(W("nWX"), qN), (n2I, xv)])
             tt(xv, p, xv, A.max)
@@ -384,19 +409,19 @@ def build(g, T, topo, core, dst):
         if ph < 2:
             p = ps(2, 400, 48)
             compact(p, Zh, zN)
-            ts(sub(offs(t + 1), 16, 64), p, 2048.0, A.add)
+            aff(sub(offs(t + 1), 16, 64), p, 1.0, 2048.0)
         if t < 5:
-            tt(sB, b, B("db"), A.add, soff=o2)
+            tt(B("bn"), b, B("db"), A.add)
+            cp(sB, B("bn"), soff=o2)
         tt(sC, cr, dl, A.add, soff=o2)
-        if t in (1, 2):
-            tt(B("rf", "ff"), r64, B("dr", "ff"), A.add)
-            act(B("rn", "ff"), B("rf", "ff"), F.Identity, bias=-2048.0, scale=1.0 / 64)
-            cp(sR, B("rn", "ff"), soff=o2)
+        if t == 2:
+            for lo in range(0, NP, 512):
+                aff(view("tabr", lo, lo + 512), view("tabc", lo, lo + 512), 1.0 / 64, -31.0 / 64 - 2048)
     yp = view("tabc", 0, NH)
     dma(T.yp[:], yp[3], NH * 512, [yp], [])
     finish([x, dx], [D4, y], 0, 3)
-    dma(T.yt[:, 0:NW], sub(out, 0, NW)[3], NW * 256, [sub(out, 0, NW)], [])
-    dma(T.yt[:, NW:NT], sub(out, NW, NT)[3], NN * 256, [sub(out, NW, NT)], [])
+    dma(T.yt[:, 0:NW], sub(out, 0, NW)[3], NW * 256, [sub(out, 0, NW)], [], "act")
+    dma(T.yt[:, NW:NT], sub(out, NW, NT)[3], NN * 256, [sub(out, NW, NT)], [], "act")
     return ops, nr[0] * neng
 
 
@@ -418,107 +443,112 @@ def links(ops):
     return deps
 
 
-def plan(ops, base=None):
+def plan(ops, base, succ, banks, path, pert):
     n = len(ops)
-    deps = [set(d) for d in (base or links(ops))]
-    lat = [0.0 if "nbytes" not in o else (CFG["rem"] if o.get("remote") else CFG["dma"]) for o in ops]
-    succ = [[] for _ in range(n)]
-    for i in range(n):
-        for j in deps[i]:
-            succ[j].append(i)
-    prio = [0.0] * n
-    for i in range(n - 1, -1, -1):
-        prio[i] = ops[i]["cost"] + lat[i] + ops[i].get("nbytes", 0) / CFG["bpn"] + max([prio[k] + CFG["hop"] for k in succ[i]] + [0.0])
-    for i in range(n):
-        prio[i] += PERT.get(i, 0.0) + (1e6 - i if ops[i]["eng"] == "sync" and not ops[i]["reads"] else 0.0)
-    eng = [o["eng"] for o in ops]
-    banks = [sorted(set(x[0] for x in o["reads"] + o["writes"] if x[0][0] == "p")) for o in ops]
-    free, done, left = {}, [0.0] * n, [len(d) for d in deps]
+    deps = [set(d) for d in base]
+    way = [pert.get(-1 - i, 0) for i in range(n)]
+    eng = [o["ways"][w][0] for o, w in zip(ops, way)]
+    prio = [path[i] + pert.get(i, 0.0) for i in range(n)]
+    free, done, left = {"dve": 0.0, "act": 0.0, "pe": 0.0, "pool": 0.0, "sync": 0.0}, [0.0] * n, [len(d) for d in deps]
     user, order, wire, since = {}, [], 0.0, [0.0] * n
+    hop, own, look = CFG["hop"], CFG["self"], CFG["look"]
     ready = [i for i in range(n) if left[i] == 0]
     while ready:
         es = []
         for i in ready:
-            t = max(free.get(eng[i], 0.0), since[i])
+            t = max(free[eng[i]], since[i])
             for bk in banks[i]:
                 for u in user.get(bk, {}).values():
-                    if eng[u] != eng[i]:
-                        t = max(t, done[u] + CFG["hop"])
+                    if eng[u] != eng[i] and done[u] + hop > t:
+                        t = done[u] + hop
             es.append((t, i))
         t0, i0 = min(es)
-        t, i = max([e for e in es if eng[e[1]] == eng[i0] and e[0] <= t0 + CFG["look"]], key=lambda e: prio[e[1]])
+        t, i = max([e for e in es if eng[e[1]] == eng[i0] and e[0] <= t0 + look], key=lambda e: prio[e[1]])
         o = ops[i]
         for bk in banks[i]:
             for u in user.get(bk, {}).values():
                 if eng[u] != eng[i]:
                     deps[i].add(u)
             user.setdefault(bk, {})[eng[i]] = i
-        free[eng[i]] = done[i] = t + o["cost"]
+        free[eng[i]] = done[i] = t + o["ways"][way[i]][1]
         if "nbytes" in o:
-            wire = max(wire, done[i] + lat[i]) + o["nbytes"] / CFG["bpn"]
+            wire = max(wire, done[i] + (CFG["rem"] if o.get("remote") else CFG["dma"])) + o["nbytes"] / CFG["bpn"]
             done[i] = wire
-        order.append((i, t, done[i]))
+        order.append(i)
         ready.remove(i)
         for k in succ[i]:
             if not (eng[k] == "pe" and eng[i] == "pe"):
-                since[k] = max(since[k], done[i] + (CFG["self"] if eng[k] == eng[i] else CFG["hop"]))
+                since[k] = max(since[k], done[i] + (own if eng[k] == eng[i] else hop))
             left[k] -= 1
             if left[k] == 0:
                 ready.append(k)
-    return order, deps
+    return order, deps, way, eng
 
 
-def replay(ops, order, deps, cfg, cost):
-    free, done, wire = {}, {}, 0.0
-    for i, _t, _d in order:
-        o = ops[i]
-        e = o["eng"]
+def replay(ops, got, cfg, cost):
+    order, deps, way, eng = got
+    free, done, wire, hop, own = {}, {}, 0.0, cfg["hop"], cfg["self"]
+    for i in order:
+        o, e = ops[i], eng[i]
         t = free.get(e, 0.0)
         for j in deps[i]:
-            f = ops[j]["eng"]
-            if f != e:
-                t = max(t, done[j] + cfg["hop"])
-            elif e != "pe":
-                t = max(t, done[j] + cfg["self"])
-        free[e] = done[i] = t + cost[i]
+            if eng[j] != e:
+                if done[j] + hop > t:
+                    t = done[j] + hop
+            elif e != "pe" and done[j] + own > t:
+                t = done[j] + own
+        free[e] = done[i] = t + cost[i][way[i]]
         if "nbytes" in o:
             wire = max(wire, done[i] + (cfg["rem"] if o.get("remote") else cfg["dma"])) + o["nbytes"] / cfg["bpn"]
             done[i] = wire
     return max(done.values())
 
 
-def shape(make):
+def shape(make, pert, rounds):
     keep, sets = dict(CFG), []
     for gs in GUESS:
         CFG.update(keep)
         CFG.update(gs)
-        sets.append((dict(CFG), [o["cost"] for o in make()]))
+        sets.append((dict(CFG), [[w[1] for w in o["ways"]] for o in make()]))
     CFG.update(keep)
     ops = make()
     base, n, seed = links(ops), len(ops), [CFG["seed"]]
+    succ = [[] for _ in range(n)]
+    for i in range(n):
+        for j in base[i]:
+            succ[j].append(i)
+    banks = [sorted(set(x[0] for x in o["reads"] + o["writes"] if x[0][0] == "p")) for o in ops]
+    twice = [i for i in range(n) if len(ops[i]["ways"]) > 1]
+    path = [0.0] * n
+    for i in range(n - 1, -1, -1):
+        o = ops[i]
+        lat = 0.0 if "nbytes" not in o else (CFG["rem"] if o.get("remote") else CFG["dma"]) + o["nbytes"] / CFG["bpn"]
+        path[i] = o["ways"][0][1] + lat + max([path[k] + CFG["hop"] for k in succ[i]] + [0.0])
+    for i in range(n):
+        if "nbytes" in ops[i] and not ops[i]["reads"]:
+            path[i] += 1e6 - 1e4 * i
 
     def draw(k):
         seed[0] = (seed[0] * 1103515245 + 12345) % 2147483648
         return (seed[0] >> 8) % k
 
     def total(p):
-        PERT.clear()
-        PERT.update(p)
-        got = plan(ops, base)
-        return sum(replay(ops, got[0], got[1], c, x) for c, x in sets), got
-    pert = {}
+        got = plan(ops, base, succ, banks, path, p)
+        return sum(replay(ops, got, c, x) for c, x in sets), got
     best, got = total(pert)
-    for _ in range(CFG["rounds"]):
+    for _ in range(rounds):
         p, a = dict(pert), draw(n)
-        for _k in range(1 << draw(3)):
-            j = min(n - 1, max(0, a + draw(61) - 30))
-            p[j] = p.get(j, 0.0) + 100.0 * (draw(21) + draw(21) - 20)
+        if draw(2):
+            j = -1 - twice[draw(len(twice))]
+            p[j] = 1 - p.get(j, 0)
+        else:
+            for _k in range(1 << draw(3)):
+                j = min(n - 1, max(0, a + draw(61) - 30))
+                p[j] = p.get(j, 0.0) + 100.0 * (draw(21) + draw(21) - 20)
         r, o = total(p)
         if r < best - 1.0:
             best, got, pert = r, o, p
-    PERT.clear()
-    PERT.update(pert)
-    return got
+    return best, got, pert
 
 
 def rank_program(g, core, T, topo):
@@ -526,18 +556,17 @@ def rank_program(g, core, T, topo):
     if rank is None:
         return
     dst = T.cores[(rank + 1) % len(T.cores)]
-    ops, nsent = build(g, T, topo, core, dst)
     if "p" not in PLAN:
-        PLAN["p"] = shape(lambda: build(g, T, topo, core, dst)[0])
-    order, deps = PLAN["p"]
+        PLAN["p"] = shape(lambda: build(g, T, topo, core, dst)[0], {}, CFG["rounds"])[1]
+    ops, nsent = build(g, T, topo, core, dst)
+    order, deps, way, eng = PLAN["p"]
     queue = {"dve": g.vector, "act": g.scalar, "pe": g.tensor, "pool": g, "sync": g.sync}
     count, mark, waited = {}, {}, {}
-    for i, _t, _d in order:
-        o = ops[i]
-        e = o["eng"]
+    for i in order:
+        o, e = ops[i], eng[i]
         need = {}
         for j in deps[i]:
-            if e == "pe" and ops[j]["eng"] == "pe":
+            if e == "pe" and eng[j] == "pe":
                 continue
             key, sem, val = mark[j]
             if val > need.get(key, (None, 0))[1]:
@@ -547,7 +576,7 @@ def rank_program(g, core, T, topo):
             if waited.get((e, key), 0) < val:
                 queue[e].wait_ge(sem, val)
                 waited[(e, key)] = val
-        ins = o["fn"]()
+        ins = o["ways"][way[i]][2]()
         if "sem" in o:
             mark[i] = ("x%d" % i, o["sem"], o["val"])
         else:

from concourse.bass import DstId, RemoteDMATransfer
from concourse.mybir import AluOpType as A, ActivationFunctionType as F, AxisListType as AX

CFG = {"cyc": 1.04, "pe": 0.52, "gat": 1.56, "sca": 3.8, "tt2": 1.0, "fix": 60.0, "hop": 120.0, "self": 60.0, "dma": 2200.0, "bpn": 250.0,
       "rem": 2500.0, "look": 60.0, "rounds": 5500, "seed": 1}
GUESS = [dict(cyc=0.9, pe=0.45, fix=40.0, hop=100.0, self=50.0), dict(cyc=1.2, pe=0.6, gat=2.05, sca=5.8),
         dict(bpn=150.0, dma=3000.0, rem=4000.0, hop=250.0), dict(tt2=2.0, gat=1.2, sca=2.5)]
PLAN = {}

NP, NT, NW, NH, WIN = 4096, 1024, 256, 2048, 6400
SCRATCH = {
    "ci": ("sbuf", [128, NP], "int32"), "tabc": ("sbuf", [128, WIN], "float32"),
    "tabr": ("sbuf", [128, NP], "int32"), "tabb": ("sbuf", [128, WIN], "int32"),
    "bf": ("sbuf", [128, 30720], "bfloat16"), "hf": ("sbuf", [128, 6144], "float16"), "ff": ("sbuf", [128, 8192], "float32"),
    "ii": ("sbuf", [128, 1024], "int32"), "uu": ("sbuf", [128, 512], "uint16"), "eq": ("sbuf", [128, 16, 256], "bfloat16"),
}
for _k in range(8):
    SCRATCH["p%d" % _k] = ("psum", [128, 512], "float32")
CUTS = [0, 512, 1152, 1792, 2432, 2944, 3456, 3840, 4096]
SEMAPHORES = ["dve", "act", "pe", "pool", "sent"] + ["d%d" % _k for _k in range(14)] + ["r%d" % _k for _k in range(4)]


def build(g, T, topo, core, dst):
    ops = []
    top = {"bf": 0, "hf": 0, "ff": 0, "ii": 0, "uu": 0}
    named = {}
    v, s, pe = g.vector, g.scalar, g.tensor
    cyc, fix = CFG["cyc"], CFG["fix"]

    def view(name, lo, hi, step=1):
        return (name, lo, hi, T[name][:, lo:hi] if step == 1 else T[name][:, lo:hi:step])

    def new(key, arena, n):
        if key not in named:
            lo = top[arena]
            top[arena] = lo + (n + 15) // 16 * 16
            assert top[arena] <= SCRATCH[arena][1][1], arena
            named[key] = view(arena, lo, lo + n)
        return named[key]

    def sub(x, lo, hi, step=1):
        return view(x[0], x[1] + lo, x[1] + hi, step)

    def ps(bank, lo, n):
        return view("p%d" % bank, lo, lo + n)

    def wid(x):
        return x[2] - x[1]

    def two(*xs):
        return all(x[0] in ("bf", "hf", "uu", "eq") for x in xs)

    def op(eng, cost, fn, reads, writes, **kw):
        ops.append(dict(ways=[(eng, cost, fn)], reads=[x for x in reads if isinstance(x, tuple)], writes=writes, **kw))

    def both():
        o = ops.pop()
        ops[-1]["ways"] += o["ways"]
        ops[-1]["reads"] += o["reads"]

    def ap(x):
        return x[3] if isinstance(x, tuple) else x

    def ind(win, off):
        return win[3].indirect(off[3])

    def act(out, in_, func, bias=0.0, scale=1.0, off=None):
        op("act", fix + max(64, wid(out) * (CFG["gat"] if off else 1.0)) * cyc,
           lambda: s.activation(out[3], ind(in_, off) if off else in_[3], func, bias=ap(bias), scale=ap(scale)), [in_, bias, scale, off], [out])

    def ts(out, in_, s1, o1, s2=None, o2=None):
        c = fix + max(64, wid(out) * (0.5 if two(out, in_) else 1.0)) * cyc
        if o2 is None:
            op("dve", c, lambda: v.tensor_scalar(out[3], in_[3], ap(s1), None, o1), [in_, s1], [out])
        else:
            op("dve", c, lambda: v.tensor_scalar(out[3], in_[3], ap(s1), ap(s2), o1, o2), [in_, s1, s2], [out])

    def cp(out, in_, off=None, soff=None):
        k = CFG["sca"] if soff else CFG["gat"]
        op("dve", fix + max(64, wid(in_ if soff else out) * k) * cyc,
           lambda: v.tensor_copy(ind(out, soff) if soff else out[3], ind(in_, off) if off else in_[3]), [in_, off, soff], [out])

    def tt(out, a, b, o, off=None, soff=None):
        if off:
            k = CFG["gat"]
        elif soff:
            k = CFG["sca"]
        elif a[0][0] == "p" or b[0][0] == "p":
            k = 1.0
        else:
            k = CFG["tt2"] if two(out, a, b) else 2.0
        op("dve", fix + max(64, wid(b) * k) * cyc,
           lambda: v.tensor_tensor(ind(out, soff) if soff else out[3], ind(a, off) if off else a[3], b[3], o), [a, b, off, soff], [out])

    def aff(out, in_, scale=1.0, bias=0.0):
        act(out, in_, F.Identity, bias=bias, scale=scale)
        ts(out, in_, scale, A.mult, bias, A.add)
        both()

    def relu(out, in_, bias):
        act(out, in_, F.Relu, bias=bias)
        ts(out, in_, bias, A.add, 0.0, A.max)
        both()

    def above(out, in_, scale, bias, k, lim):
        act(out, in_, F.Sigmoid, bias=bias, scale=scale)
        ts(out, in_, k, A.mult, lim, A.is_gt)
        both()

    def pick(out, win, off):
        act(out, win, F.Copy, off=off)
        cp(out, win, off=off)
        both()

    def mm(out, terms, start=True, stop=True):
        c = sum(max(64, wid(out)) for w, r in terms) * CFG["pe"] + 30

        def fn():
            last = None
            for k, (w, r) in enumerate(terms):
                last = pe.matmul(out[3], w[3], r[3], start and k == 0, stop and k == len(terms) - 1)
            return last
        op("pe", c, fn, [x for t in terms for x in t] + ([] if start else [out]), [out])

    def compact(out, z, src, extra=()):
        mm(out, list(extra) + [(sub(z, 15 - i, 143 - i), sub(src, i, wid(src), 16)) for i in range(16)])

    def sel(out, in_, pattern, cmp, base, mult, fill=0.0):
        op("pool", 170 + 2 * wid(out) * cyc, lambda: g.affine_select(out[3], in_[3], pattern, cmp, fill, base, mult), [in_], [out])

    def fill(out, c):
        op("dve", fix + max(64, wid(out) * 0.5) * cyc, lambda: v.memset(out[3], c), [], [out])

    nd, nr = [0], [0]

    def dma(out, in_, nbytes, reads, writes, eng="sync"):
        sem = T.sem["d%d" % nd[0]]
        nd[0] += 1
        op(eng, 80, lambda: (g.sync if eng == "sync" else s).dma_start(out, in_).then_inc(sem, 16), reads, writes, sem=sem, val=16, nbytes=nbytes)

    rid, pid, _se = topo.addr(dst)
    mask = topo.mask(core, dst)
    neng = len(topo.engines(core, dst))

    def send(land, srcs):
        sem = T.sem["r%d" % nr[0]]
        nr[0] += 1
        if len(srcs) == 1:
            fn = lambda: g.remote_dma(land[3], srcs[0][3], sem, T.sem.sent, pid, rid, mask)
        else:
            fn = lambda: g.remote_dma_fused([RemoteDMATransfer(dst_ids=[DstId(rid=rid, pnc=pid)], dma_engine_mask=mask, remote_sem=sem,
                                                               srcs=[x[3] for x in srcs], dsts=[land[3]], alu_op=1)], local_sem=T.sem.sent)
        op("pool", 300, fn, srcs, [land], sem=sem, val=neng, remote=True, nbytes=wid(land) * 256 * len(srcs))

    trav = new("trav", "bf", NT)
    wi, thi = new("wi", "ii", 1), new("thi", "ii", 1)
    cuts = list(zip(CUTS, CUTS[1:]))
    for k, (lo, hi) in enumerate(cuts):
        c = view("ci", lo, hi)
        dma(c[3], T.peers[:, lo:hi], (hi - lo) * 512, [], [c])
        if k == 0:
            dma(trav[3], T.trav[:], NT * 256, [], [trav], "act")
            dma(wi[3], T.wts[:], 512, [], [wi], "act")
            dma(thi[3], T.th[:], 512, [], [thi], "act")

    def W(key, arena="bf", n=128):
        return new("W" + key, arena, n)
    one = W("one", "bf", 256)
    fill(one, 1.0)
    o128 = sub(one, 0, 128)
    sel(W("I"), o128, [[-1, 128]], A.is_equal, 0, 1)
    sel(W("b0"), o128, [[-16, 8], [0, 16]], A.is_ge, 0, 1)
    sel(W("Blk"), W("b0"), [[16, 8], [0, 16]], A.is_ge, 15, -1)
    sel(W("L"), W("Blk"), [[1, 128]], A.is_gt, 0, -1)
    sel(W("U"), W("Blk"), [[-1, 128]], A.is_gt, 0, 1)
    h0, h1, h2, thr = (W(key, "bf", 256) for key in ("h0", "h1", "h2", "thr"))
    sel(h0, one, [[0, 16], [1, 16]], A.is_gt, 0, 0)
    aff(h1, h0, -2.0, 2.0)
    aff(h2, h0, 0.5)
    op("dve", fix + 128 * cyc, lambda: v.tensor_tensor_scan(thr[3], h2[3], h1[3], 0.0, A.mult, A.add), [h2, h1], [thr])
    Z = W("Z", "bf", 144)
    fill(Z, 0.0)
    op("dve", fix + 64 * cyc, lambda: v.tensor_copy(sub(Z, 15, 143, 16)[3], sub(W("Blk"), 0, 128, 16)[3]), [W("Blk"), Z], [Z])
    for key, src, c, arena in (("nI", "I", -1.0, "bf"), ("n2I", "I", -2.0, "bf"), ("nhI", "I", -0.5, "bf"), ("hI", "I", 0.5, "bf"),
                               ("I256", "I", 256.0, "bf"), ("L4", "L", 4.0, "bf"), ("nL4", "L", -4.0, "bf"), ("Blk64", "Blk", 64.0, "bf"),
                               ("BlkS", "Blk", 1.0 / 2048, "bf"), ("U16", "U", 16.0, "bf"),
                               ("Blkh", "Blk", 1.0, "hf"), ("I64h", "I", 64.0, "hf"), ("nI64h", "I", -64.0, "hf")):
        aff(W(key, arena), W(src), c)
    for key, src, c in (("Wval", "nL4", 1.0), ("WX", "L4", 1.0), ("nWX", "nL4", -1.0)):
        sel(W(key), W(src), [[-1, 128]], A.not_equal, 0, 1, c)
    Zh, Z256, Zw = W("Zh", "hf", 144), W("Z256", "bf", 144), W("Zw", "bf", 144)
    aff(Zh, Z)
    aff(Z256, Z, 256.0)
    col = lambda key: new("c" + key, "ff", 1)
    tt(W("tmp"), W("I"), sub(thr, 0, 128), A.mult)
    op("dve", fix + 128 * cyc, lambda: v.tensor_reduce(col("p2")[3], W("tmp")[3], AX.X, A.add), [W("tmp")], [col("p2")])
    op("dve", fix + 128 * cyc, lambda: v.tensor_reduce(col("lev")[3], W("U")[3], AX.X, A.add), [W("U")], [col("lev")])
    aff(col("p1"), col("p2"), 0.5)
    aff(W("Wd"), W("Blk"), col("p1"))
    act(col("last"), col("lev"), F.Sigmoid, bias=-14.5 * 256, scale=256.0)
    aff(col("at"), col("last"), 256.0, -128.0)
    aff(col("al"), col("last"), -1.0, 0.5)
    j16, jc = new("j16", "ff", 16), new("jc", "bf", 16)
    op("pool", 160, lambda: g.iota(j16[3], [[16, 16]], 0, 0, allow_small_or_imprecise_dtypes=True), [], [j16])
    aff(jc, j16, 1.0, col("lev"))
    aff(col("w"), wi, 0.25)
    aff(col("k"), thi, -256.0, -64.0 * 7166)
    aff(col("kl"), thi, 4.0, 7166.0)
    aff(Zw, Z, col("w"))
    aff(W("Blkw"), W("Blk"), col("w"))
    I, nI, n2I, WX, I256 = W("I"), W("nI"), W("n2I"), W("WX"), W("I256")

    NN = NT - NW
    parts = [(0, NN // 2), (NN // 2, NN)]
    st = new("st0", "bf", 2 * NW)
    xN, DN = new("xN0", "bf", NN), new("DN0", "bf", NN)
    xN1, DN1, st3 = new("xN1", "bf", NN), new("DN1", "bf", NN), new("st3", "bf", 2 * NW)
    tmp = new("tmpT", "bf", NT)
    pieces = [(sub(trav, 0, NW), sub(st, 0, NW), sub(st, NW, 2 * NW), sub(tmp, 0, NW), 3)]
    pieces += [(sub(trav, NW + a, NW + b), sub(xN, a, b), sub(DN, a, b), sub(tmp, NW + a, NW + b), k) for k, (a, b) in enumerate(parts)]
    for sv, xv, dv, tv, bank in pieces:
        aff(tv, sv, 0.25, 191.75)
        aff(dv, tv, 4.0, -768.0)
        pa = ps(bank, 0, wid(sv))
        mm(pa, [(I, sv), (nI, dv)])
        act(tv, pa, F.Abs, bias=-2.5, scale=2.0)
        aff(xv, tv, -1.0, 1.5)
    send(DN1, [DN])

    def offs(t):
        return new("off%d" % t, "uu", 64)

    def first(t, dv, p, lo, hi):
        compact(p, Zw, dv)
        a, b = new("fa%d" % lo, "ii", hi - lo), new("fb%d" % lo, "ii", hi - lo)
        aff(a, p)
        ts(b, a, NP - 1, A.bitwise_and)
        aff(sub(offs(t), lo, hi), b)
        return b

    def first_w(t, dv):
        aff(new("mcf%d" % t, "ff", 16), first(t, dv, ps(2, 448, 16), 0, 16), 1.0, -2048.0)
        p = ps(7, 256, NW)
        mm(p, [(W("Blkw"), dv)])
        a, b = new("fw3", "ii", NW), new("fw4", "ii", NW)
        aff(a, p)
        ts(b, a, NP - 1, A.bitwise_and)
        aff(new("M%d" % t, "hf", NW), b, 1.0, -2048.0)

    first_w(0, sub(st, NW, 2 * NW))
    first(0, DN, ps(2, 400, 48), 16, 64)

    for lo, hi in cuts:
        c = view("ci", lo, hi)
        aff(view("tabc", lo, hi), c)
        ts(view("tabb", lo, hi), c, 3, A.bitwise_and)
        aff(view("tabr", lo, hi), c, 1.0 / 64, -31.0 / 64 - 2048)
    gB, gR, gC = view("tabb", 0, NP), view("tabr", 0, NP), view("tabc", 0, NP)
    sB, sC = view("tabb", 0, WIN), view("tabc", 0, WIN)
    out = new("out", "bf", NT)

    def finish(xs, ds, lo, bank):
        n = wid(xs[0])
        y0, p = sub(tmp, lo, lo + n), ps(bank, 0, n)
        if len(xs) > 1:
            mm(p, [(I, u) for u in xs])
        act(y0, p if len(xs) > 1 else xs[0], F.Abs, bias=0.5, scale=-2.0)
        mm(p, [(I, u) for u in ds] + [(nI, y0)])
        aff(sub(out, lo, lo + n), p, 1.0, 2.5)

    for t in range(6):
        ph, par = t % 3, t % 2
        B = lambda key, arena="bf", n=NW: new("%s%d" % (key, par), arena, n)
        if t == 3:
            first(3, DN1, ps(2, 400, 48), 16, 64)
            st, xN, DN = st3, xN1, DN1
            first_w(3, sub(st3, NW, 2 * NW))
        x, D4 = sub(st, 0, NW), sub(st, NW, 2 * NW)
        ch = new("ch%d" % t, "bf", 2 * NW)
        dx, y = sub(ch, 0, NW), sub(ch, NW, 2 * NW)
        off, M, mcf = offs(t), new("M%d" % t, "hf", NW), new("mcf%d" % t, "ff", 16)
        oW = sub(off, 0, 16)
        b, q = B("b"), B("q")
        pick(b, gB, oW)
        p = ps(3, 0, NW)
        mm(p, [(I, x), (I, b)])
        act(q, p, F.Abs, bias=-2.0)
        pv = ps(4, 0, NW)
        cr, r64, r16 = B("cr", "ff"), B("r64", "ff"), B("r16", "hf")
        pick(cr, gC, oW)
        if t in (0, 1, 4):
            act(r64, gR, F.Identity, bias=64.0 * 2048, scale=64.0, off=oW)
            rs = (r64, 1.0 / 64, -2048.0)
        else:
            ri = new("ri", "ii", NW)
            aff(ri, cr, 1.0 / 64, -31.0 / 64)
            aff(r64, ri, 64.0)
            rs = (ri, 1.0, -2048.0)
        if t:
            aff(r16, *rs)
        if ph < 2:
            mm(pv, [(W("Wval"), q)])
            above(B("at"), pv, 256.0, col("at"), 1.0, col("al"))
            z = B("z", "hf")
            if t:
                tt(z, r16, B("at"), A.mult)
            else:
                tt(z, gR, B("at"), A.mult, off=oW)
            p = ps(2, 448, 16)
            compact(p, Zh, z)
            aff(sub(offs(t + 1), 0, 16), p, 1.0, 2048.0)
            aff(new("mcf%d" % (t + 1), "ff", 16), p)
            p = ps(7, 256, NW)
            mm(p, [(W("Blkh", "hf"), z)])
            aff(new("M%d" % (t + 1), "hf", NW), p)
        tt(B("s"), gC, r64, A.subtract, off=oW)
        pu = ps(6, 0, NW)
        mm(pu, [(nI, D4), (nI, b), (I, B("s"))])
        act(B("au"), pu, F.Abs)
        relu(B("ru"), pu, 0.0)
        pc = ps(5, 0, NW)
        mm(pc, [(nI, thr)], True, False)
        for c in range(16):
            n = NW - 16 * c
            e = ("eq", c * 256, c * 256 + n, T.eq[:, c, 0:n])
            ts(e, sub(M, 16 * c, NW), sub(mcf, c, c + 1), A.is_equal)
            if c < 15:
                mm(sub(pc, 16 * c + 16, NW), [(W("Blk64"), ("eq", c * 256 + 16, c * 256 + n, T.eq[:, c, 16:n]))], False, False)
        mm(pc, [(W("Wd"), ("eq", 0, 4096, T.eq[:, :, 0:16]))], False, True)
        tw = B("tw")
        act(tw, pc, F.Sign, bias=2.0 ** -16)
        pk = ps(4, 256, NW)
        mm(pk, [(W("Wval"), q), (W("BlkS"), B("au")), (W("nhI"), tw)])
        k1 = B("k1")
        above(k1, pk, 131072.0, col("k"), 2048.0, col("kl"))
        p = ps(3, 256, NW)
        mm(p, [(WX, q), (I256, x), (n2I, k1)])
        act(dx, p, F.Relu, bias=-253.0, scale=-1.0)
        p = ps(6, 256, NW)
        mm(p, [(I, B("ru")), (W("Blk64"), k1)])
        relu(y, p, -64.0)
        if t == 2:
            send(st3, [st, ch])
        p = ps(3, 0, NW)
        mm(p, [(WX, q), (I256, b), (n2I, k1)])
        act(B("db"), p, F.Relu, bias=3.0, scale=-1.0)
        p = ps(2, 464, 16)
        compact(p, Z256, tw, [(I, jc)])
        tt(B("o2", "ff", 16), p, mcf, A.max)
        o2 = B("off2", "uu", 16)
        aff(o2, B("o2", "ff", 16), 1.0, 2048.0)
        kap = new("kap%d" % ph, "bf", NW)
        if ph < 2:
            act(kap, dx, F.Sign)
            ts(kap, dx, 0.5, A.is_gt)
            both()
        dl = B("dl", "ff")
        if ph == 0:
            p = ps(3, 256, NW)
            mm(p, [(I, B("db")), (nI, y)])
            aff(dl, p)
        else:
            p = ps(7, 0, NW)
            mm(p, [(WX, q), (W("hI"), x), (W("nhI"), b), (I256, tw)])
            ts(B("k4"), p, -255.5, A.is_equal)
            held = [(I256, new("kap%d" % k, "bf", NW)) for k in range(ph)]
            mm(pv, held + [(W("Wval"), q), (n2I, b), (W("U16"), B("k4"))])
            above(B("mu"), pv, 256.0, -256.0 * 256, 1.0, 256.0)
            M1 = new("M%d" % (t - ph), "hf", NW)
            p1, p2, p3 = (new(u, "hf", NW) for u in ("pp1", "pp2", "pp3"))
            pu = ps(7, 256, NW)
            mm(pu, [(W("I64h", "hf"), u) for u in ([M1] if ph == 1 else [p1, p2, p3])] + [(W("nI64h", "hf"), r16)])
            dr = B("dr", "ff")
            tt(dr, pu, B("mu"), A.mult)
            p = ps(3, 256, NW)
            mm(p, [(I, B("db")), (nI, y)])
            tt(dl, p, dr, A.add)
            if ph == 1:
                above(B("nu"), pv, 256.0, -262.0 * 256, 1.0, 262.0)
                tt(p1, r16, B("nu"), A.mult)
                tt(B("om"), new("kap0", "bf", NW), B("nu"), A.subtract)
                tt(p3, M1, B("om"), A.mult)
                tt(p2, M, kap, A.mult)
        if ph < 2:
            stn = new("sn%d" % t, "bf", 2 * NW)
            tt(sub(stn, 0, NW), x, dx, A.add)
            tt(sub(stn, NW, 2 * NW), D4, y, A.add)
            st = stn
        zN = B("zN", "hf", NN)
        for k, (lo, hi) in enumerate(parts):
            n = hi - lo
            oN, xv = sub(off, 16 + lo // 16, 16 + hi // 16), sub(xN, lo, hi)
            bN, qN = (sub(B(key, "bf", NN), lo, hi) for key in ("bN", "qN"))
            p = ps(k, 0, n)
            pick(bN, gB, oN)
            mm(p, [(I, xv), (I, bN)])
            act(qN, p, F.Abs, bias=-2.0)
            if ph < 2:
                aN, pv2 = sub(B("aN", "bf", NN), lo, hi), ps(2, 0, n)
                mm(pv2, [(W("Wval"), qN)])
                above(aN, pv2, 256.0, col("at"), 1.0, col("al"))
                tt(sub(zN, lo, hi), gR, aN, A.mult, off=oN)
            mm(p, [(W("nWX"), qN), (n2I, xv)])
            tt(xv, p, xv, A.max)
            if t == 2:
                send(sub(xN1, lo, hi), [xv])
            if t == 5:
                finish([xv], [sub(DN, lo, hi)], NW + lo, k)
        if ph < 2:
            p = ps(2, 400, 48)
            compact(p, Zh, zN)
            aff(sub(offs(t + 1), 16, 64), p, 1.0, 2048.0)
        if t < 5:
            tt(B("bn"), b, B("db"), A.add)
            cp(sB, B("bn"), soff=o2)
        tt(sC, cr, dl, A.add, soff=o2)
        if t == 2:
            for lo in range(0, NP, 512):
                aff(view("tabr", lo, lo + 512), view("tabc", lo, lo + 512), 1.0 / 64, -31.0 / 64 - 2048)
    yp = view("tabc", 0, NH)
    dma(T.yp[:], yp[3], NH * 512, [yp], [])
    finish([x, dx], [D4, y], 0, 3)
    dma(T.yt[:, 0:NW], sub(out, 0, NW)[3], NW * 256, [sub(out, 0, NW)], [], "act")
    dma(T.yt[:, NW:NT], sub(out, NW, NT)[3], NN * 256, [sub(out, NW, NT)], [], "act")
    return ops, nr[0] * neng


def links(ops):
    deps = [set() for _ in ops]
    seen = {}
    for i, o in enumerate(ops):
        for kind, lst in (("r", o["reads"]), ("w", o["writes"])):
            for x in lst:
                for (j, k2, lo, hi) in seen.get(x[0], []):
                    if j != i and lo < x[2] and x[1] < hi and (kind == "w" or k2 == "w"):
                        deps[i].add(j)
        for kind, lst in (("r", o["reads"]), ("w", o["writes"])):
            for x in lst:
                rest = seen.get(x[0], [])
                if kind == "w":
                    rest = [e for e in rest if not (x[1] <= e[2] and e[3] <= x[2])]
                seen[x[0]] = rest + [(i, kind, x[1], x[2])]
    return deps


def plan(ops, base, succ, banks, path, pert):
    n = len(ops)
    deps = [set(d) for d in base]
    way = [pert.get(-1 - i, 0) for i in range(n)]
    eng = [o["ways"][w][0] for o, w in zip(ops, way)]
    prio = [path[i] + pert.get(i, 0.0) for i in range(n)]
    free, done, left = {"dve": 0.0, "act": 0.0, "pe": 0.0, "pool": 0.0, "sync": 0.0}, [0.0] * n, [len(d) for d in deps]
    user, order, wire, since = {}, [], 0.0, [0.0] * n
    hop, own, look = CFG["hop"], CFG["self"], CFG["look"]
    ready = [i for i in range(n) if left[i] == 0]
    while ready:
        es = []
        for i in ready:
            t = max(free[eng[i]], since[i])
            for bk in banks[i]:
                for u in user.get(bk, {}).values():
                    if eng[u] != eng[i] and done[u] + hop > t:
                        t = done[u] + hop
            es.append((t, i))
        t0, i0 = min(es)
        t, i = max([e for e in es if eng[e[1]] == eng[i0] and e[0] <= t0 + look], key=lambda e: prio[e[1]])
        o = ops[i]
        for bk in banks[i]:
            for u in user.get(bk, {}).values():
                if eng[u] != eng[i]:
                    deps[i].add(u)
            user.setdefault(bk, {})[eng[i]] = i
        free[eng[i]] = done[i] = t + o["ways"][way[i]][1]
        if "nbytes" in o:
            wire = max(wire, done[i] + (CFG["rem"] if o.get("remote") else CFG["dma"])) + o["nbytes"] / CFG["bpn"]
            done[i] = wire
        order.append(i)
        ready.remove(i)
        for k in succ[i]:
            if not (eng[k] == "pe" and eng[i] == "pe"):
                since[k] = max(since[k], done[i] + (own if eng[k] == eng[i] else hop))
            left[k] -= 1
            if left[k] == 0:
                ready.append(k)
    return order, deps, way, eng


def replay(ops, got, cfg, cost):
    order, deps, way, eng = got
    free, done, wire, hop, own = {}, {}, 0.0, cfg["hop"], cfg["self"]
    for i in order:
        o, e = ops[i], eng[i]
        t = free.get(e, 0.0)
        for j in deps[i]:
            if eng[j] != e:
                if done[j] + hop > t:
                    t = done[j] + hop
            elif e != "pe" and done[j] + own > t:
                t = done[j] + own
        free[e] = done[i] = t + cost[i][way[i]]
        if "nbytes" in o:
            wire = max(wire, done[i] + (cfg["rem"] if o.get("remote") else cfg["dma"])) + o["nbytes"] / cfg["bpn"]
            done[i] = wire
    return max(done.values())


def shape(make, pert, rounds):
    keep, sets = dict(CFG), []
    for gs in GUESS:
        CFG.update(keep)
        CFG.update(gs)
        sets.append((dict(CFG), [[w[1] for w in o["ways"]] for o in make()]))
    CFG.update(keep)
    ops = make()
    base, n, seed = links(ops), len(ops), [CFG["seed"]]
    succ = [[] for _ in range(n)]
    for i in range(n):
        for j in base[i]:
            succ[j].append(i)
    banks = [sorted(set(x[0] for x in o["reads"] + o["writes"] if x[0][0] == "p")) for o in ops]
    twice = [i for i in range(n) if len(ops[i]["ways"]) > 1]
    path = [0.0] * n
    for i in range(n - 1, -1, -1):
        o = ops[i]
        lat = 0.0 if "nbytes" not in o else (CFG["rem"] if o.get("remote") else CFG["dma"]) + o["nbytes"] / CFG["bpn"]
        path[i] = o["ways"][0][1] + lat + max([path[k] + CFG["hop"] for k in succ[i]] + [0.0])
    for i in range(n):
        if "nbytes" in ops[i] and not ops[i]["reads"]:
            path[i] += 1e6 - 1e4 * i

    def draw(k):
        seed[0] = (seed[0] * 1103515245 + 12345) % 2147483648
        return (seed[0] >> 8) % k

    def total(p):
        got = plan(ops, base, succ, banks, path, p)
        return sum(replay(ops, got, c, x) for c, x in sets), got
    best, got = total(pert)
    for _ in range(rounds):
        p, a = dict(pert), draw(n)
        if draw(2):
            j = -1 - twice[draw(len(twice))]
            p[j] = 1 - p.get(j, 0)
        else:
            for _k in range(1 << draw(3)):
                j = min(n - 1, max(0, a + draw(61) - 30))
                p[j] = p.get(j, 0.0) + 100.0 * (draw(21) + draw(21) - 20)
        r, o = total(p)
        if r < best - 1.0:
            best, got, pert = r, o, p
    return best, got, pert


def rank_program(g, core, T, topo):
    rank = T.rank_of(core)
    if rank is None:
        return
    dst = T.cores[(rank + 1) % len(T.cores)]
    if "p" not in PLAN:
        PLAN["p"] = shape(lambda: build(g, T, topo, core, dst)[0], {}, CFG["rounds"])[1]
    ops, nsent = build(g, T, topo, core, dst)
    order, deps, way, eng = PLAN["p"]
    queue = {"dve": g.vector, "act": g.scalar, "pe": g.tensor, "pool": g, "sync": g.sync}
    count, mark, waited = {}, {}, {}
    for i in order:
        o, e = ops[i], eng[i]
        need = {}
        for j in deps[i]:
            if e == "pe" and eng[j] == "pe":
                continue
            key, sem, val = mark[j]
            if val > need.get(key, (None, 0))[1]:
                need[key] = (sem, val)
        for key in sorted(need):
            sem, val = need[key]
            if waited.get((e, key), 0) < val:
                queue[e].wait_ge(sem, val)
                waited[(e, key)] = val
        ins = o["ways"][way[i]][2]()
        if "sem" in o:
            mark[i] = ("x%d" % i, o["sem"], o["val"])
        else:
            count[e] = count.get(e, 0) + 1
            ins.then_inc(T.sem[e], 1)
            mark[i] = (e, T.sem[e], count[e])
    for e in sorted(count):
        g.wait_ge(T.sem[e], count[e])
    g.wait_ge(T.sem.sent, nsent)
    for o in ops:
        if "sem" in o:
            g.wait_ge(o["sem"], o["val"])
